import numpy as np
import ml_dtypes


def mxq(x, axis, fmt="e4m3"):
    dtype, down = {"e4m3": (ml_dtypes.float8_e4m3fn, 7), "e5m2": (ml_dtypes.float8_e5m2, 14)}[fmt]
    v = np.moveaxis(np.asarray(x, np.float32).astype(ml_dtypes.bfloat16).astype(np.float64), axis, -1)
    blocks = v.reshape(v.shape[:-1] + (-1, 32))
    amax = np.abs(blocks).max(-1, keepdims=True)
    byte = np.maximum(np.where(amax > 0, np.frexp(amax)[1] - 1 + 127, 0) - down, 1)
    scale = np.exp2(byte - 127.0)
    codes = (blocks / scale).astype(np.float32).astype(dtype).astype(np.float64)
    return np.moveaxis((codes * scale).reshape(v.shape), -1, axis)


WIDE = False


def mx_kscale(k):
    if not WIDE:
        return np.ones(k)
    levels = np.array([10, -10, 5, -5, 0])
    if k % 512:
        return np.exp2(np.random.permutation(np.resize(levels, k // 32))).repeat(32)
    a = np.empty((k // 512, 16))
    for p in range(k // 512):
        a[p, :8] = np.random.permutation(np.resize(levels, 8))
        for g in range(8):
            far = levels[np.abs(levels - a[p, g]) >= 10]
            a[p, g + 8] = far[np.random.randint(len(far))]
    return np.exp2(a.ravel()).repeat(32)


def f64(x):
    return np.asarray(x).astype(np.float64)


E2M1 = np.array([0.0, 0.5, 1.0, 1.5, 2.0, 3.0, 4.0, 6.0, -0.0, -0.5, -1.0, -1.5, -2.0, -3.0, -4.0, -6.0])


def pack_weight(w, fmt):
    k, n = w.shape
    w = f64(np.asarray(w, np.float32).astype(ml_dtypes.bfloat16)).reshape(k // 32, 32, n)
    amax = np.abs(w).max(1)
    if fmt == "e4m3":
        byte = np.frexp(amax)[1] - 1 + 127 - 7
    else:
        mant, ex = np.frexp(amax / 6.0)
        byte = np.where(mant > 0.5, ex, ex - 1) + 127
    byte = np.clip(np.where(amax > 0, byte, 1), 1, 254)
    scaled = (w * np.exp2(127.0 - byte)[:, None, :]).reshape(k, n).astype(np.float32)
    by_word = np.ascontiguousarray(scaled.reshape(k // 512, 128, 4, n).transpose(0, 1, 3, 2))
    if fmt == "e4m3":
        words = by_word.astype(ml_dtypes.float8_e4m3fn).view(np.uint8)
    else:
        c = by_word.astype(ml_dtypes.float4_e2m1fn).view(np.uint8) & 0xF
        words = (c[..., 0::2] | (c[..., 1::2] << 4)).reshape(k // 512, 128, 2 * n)
    return np.ascontiguousarray(words), np.ascontiguousarray(byte.astype(np.uint8).reshape(k // 512, 16, n))


def unpack_weight(words, scales, fmt):
    g, _, n = scales.shape
    words = np.ascontiguousarray(words).reshape(g, 128, n, -1)
    if fmt == "e4m3":
        vals = words.view(ml_dtypes.float8_e4m3fn).astype(np.float64)
    else:
        nib = np.empty((g, 128, n, 4), np.uint8)
        nib[..., 0::2] = words & 0xF
        nib[..., 1::2] = words >> 4
        vals = E2M1[nib]
    vals = vals * np.repeat(np.exp2(scales.astype(np.float64) - 127.0), 8, axis=1)[..., None]
    return vals.transpose(0, 1, 3, 2).reshape(g * 512, n)


O, T, D, Q = 512, 1024, 1024, 512


def setup_inputs():
    n = np.random.standard_normal
    s = mx_kscale(T)[:, None]
    v = n((T, D)) / s
    l = 1.5 * n((T, Q))
    p_v4 = pack_weight(v[:O], "e2m1")
    p_v8 = pack_weight(v[O:], "e4m3")
    return {
        "lg": (l - l.max(0)).astype(np.float32),
        "vs": (np.random.uniform(0.5, 2.0, T) * s[:, 0]).astype(np.float32),
        "v4_words": p_v4[0],
        "v4_scales": p_v4[1],
        "v8_words": p_v8[0],
        "v8_scales": p_v8[1],
    }


def reference(lg, vs, v4_words, v4_scales, v8_words, v8_scales):
    e_ = mxq(np.exp(f64(lg)) * f64(vs)[:, None], 0, "e4m3")
    v4_ = unpack_weight(v4_words, v4_scales, "e2m1")
    v8_ = unpack_weight(v8_words, v8_scales, "e4m3")
    y = e_[:O].T @ v4_ + e_[O:].T @ v8_
    return y

@@ -1,0 +1,171 @@
+from contextlib import ExitStack
+
+import concourse.mybir as mybir
+
+T, J, D = 1024, 512, 1024
+P = 128
+PACK = 4
+HALF = P * PACK
+J_TILE = 128
+N_TILE = 512
+
+FLOPS = 2 * T * J * D
+
+F32 = mybir.dt.float32
+BF16 = mybir.dt.bfloat16
+I32 = mybir.dt.int32
+U32 = mybir.dt.uint32
+U8 = mybir.dt.uint8
+FP8X4 = mybir.dt.float8_e4m3fn_x4
+FP4X4 = mybir.dt.float4_e2m1fn_x4
+EXP = mybir.ActivationFunctionType.Exp
+MULT = mybir.AluOpType.mult
+
+
+def tile_mix_kvmix_tm_none_kernel(tc, lg, vs, v4_words, v4_scales, v8_words, v8_scales, out):
+    nc = tc.nc
+    j_tiles = J // J_TILE
+    n_tiles = D // N_TILE
+
+    with ExitStack() as ctx:
+        keep = ctx.enter_context(tc.tile_pool(name="keep", bufs=1))
+        psum = ctx.enter_context(tc.psum_pool(name="psum", bufs=1))
+        ctx.enter_context(tc.manual_schedule())
+
+        warm = keep.tile([P, 1], F32, name="warm")
+        warmed = keep.tile([P, 1], F32, name="warmed")
+        vs_sb = keep.tile([P, 2, PACK], F32, name="vs_sb")
+        logits = [keep.tile([P, PACK, J], F32, name="logits%d" % h) for h in range(2)]
+        exps = [keep.tile([P, PACK, J], F32, name="exps%d" % h) for h in range(2)]
+        grouped = [keep.tile([P, J * PACK], BF16, name="grouped%d" % h, align_bytes=64) for h in range(2)]
+        e_codes = [keep.tile([P, J], U32, name="e_codes%d" % h, align_bytes=64) for h in range(2)]
+        e_scales = [keep.tile([P, J], U8, name="e_scales%d" % h, align_bytes=64) for h in range(2)]
+        v4_sb = keep.tile([P, 2 * D], U8, name="v4_sb", align_bytes=64)
+        v8_sb = keep.tile([P, D], U32, name="v8_sb", align_bytes=64)
+        v_scales = [keep.tile([P, D], U8, name="v_scales%d" % h, align_bytes=64) for h in range(2)]
+        results = [keep.tile([P, D], F32, name="results%d" % j) for j in range(j_tiles)]
+        accs = [
+            [psum.tile([P, N_TILE], F32, name="acc%d_%d" % (j, n)) for n in range(n_tiles)] for j in range(j_tiles)
+        ]
+
+        def load_logits(h, j0, j1):
+            rows = lg[h * HALF : (h + 1) * HALF, j0:j1].rearrange("(p i) j -> p i j", i=PACK)
+            nc.sync.dma_start(out=logits[h][:, :, j0:j1], in_=rows)
+
+        def load_scales(engine, h, scales):
+            for q in range(4):
+                engine.dma_start(
+                    out=v_scales[h][32 * q : 32 * q + 4, :].bitcast(I32),
+                    in_=scales[0, 4 * q : 4 * q + 4, :].bitcast(I32),
+                )
+
+        nc.vector.memset(warm[:], 0.0)
+        nc.vector.memset(v_scales[0][:].bitcast(I32), 0)
+        nc.vector.memset(v_scales[1][:].bitcast(I32), 0)
+        def load_v8(n):
+            cols = slice(n * N_TILE, (n + 1) * N_TILE)
+            nc.sync.dma_start(
+                out=v8_sb[:, cols].bitcast(I32),
+                in_=v8_words[0].rearrange("p n t -> p (n t)")[:, 4 * n * N_TILE : 4 * (n + 1) * N_TILE].bitcast(I32),
+            )
+
+        nc.scalar.dma_start(out=vs_sb[:], in_=vs.rearrange("(h p i) -> p h i", h=2, i=PACK))
+        load_logits(0, 0, 384)
+        load_scales(nc.scalar, 0, v4_scales)
+        nc.scalar.activation(out=warmed[:], in_=warm[:], func=EXP)
+        load_logits(1, 0, 384)
+        nc.sync.dma_start(out=v4_sb[:].bitcast(I32), in_=v4_words[0].bitcast(I32))
+        load_scales(nc.sync, 1, v8_scales)
+        load_logits(0, 384, 512)
+        load_v8(0)
+        load_v8(1)
+        load_logits(1, 384, 512)
+
+        def cols(j0, j1, per=1):
+            return slice(per * j0 * J_TILE, per * j1 * J_TILE)
+
+        def exponentiate(h, j0, j1):
+            nc.scalar.activation(out=exps[h][:, :, cols(j0, j1)], in_=logits[h][:, :, cols(j0, j1)], func=EXP)
+
+        def scale(h, j0, j1):
+            pairs = (j1 - j0) * J_TILE // 2
+            factor = vs_sb[:, h, :].unsqueeze(1).unsqueeze(3).to_broadcast([P, pairs, PACK, 2])
+            nc.vector.tensor_tensor(
+                out=grouped[h][:, cols(j0, j1, PACK)].rearrange("p (c u i) -> p c i u", u=2, i=PACK),
+                in0=exps[h][:, :, cols(j0, j1)].rearrange("p i (c u) -> p c i u", u=2),
+                in1=factor,
+                op=MULT,
+            )
+
+        def quantize(h, j0, j1):
+            nc.vector.quantize_mx(
+                out=e_codes[h][:, cols(j0, j1)].bitcast(FP8X4),
+                scales=e_scales[h][:, cols(j0, j1)],
+                in_=grouped[h][:, cols(j0, j1, PACK)],
+            )
+
+        def multiply(h, j0, j1):
+            for j in range(j0, j1):
+                for n in range(n_tiles):
+                    if h == 0:
+                        moving = v4_sb[:, 2 * n * N_TILE : 2 * (n + 1) * N_TILE].bitcast(FP4X4)
+                    else:
+                        moving = v8_sb[:, n * N_TILE : (n + 1) * N_TILE].bitcast(FP8X4)
+                    nc.tensor.matmul_mx(
+                        out=accs[j][n][:],
+                        lhsT=e_codes[h][:, cols(j, j + 1)].bitcast(FP8X4),
+                        lhsT_scale=e_scales[h][:, cols(j, j + 1)],
+                        rhs=moving,
+                        rhs_scale=v_scales[h][:, n * N_TILE : (n + 1) * N_TILE],
+                        start=(h == 0),
+                        stop=(h == 1),
+                    )
+
+        def drain(j, n, engine):
+            d_cols = slice(n * N_TILE, (n + 1) * N_TILE)
+            if engine == "scalar":
+                nc.scalar.copy(out=results[j][:, d_cols], in_=accs[j][n][:])
+            else:
+                nc.vector.tensor_copy(out=results[j][:, d_cols], in_=accs[j][n][:])
+            nc.sync.dma_start(out=out[j * J_TILE : (j + 1) * J_TILE, d_cols], in_=results[j][:, d_cols])
+
+        exponentiate(0, 0, 1)
+        exponentiate(0, 1, 2)
+        scale(0, 0, 1)
+        exponentiate(0, 2, 3)
+        scale(0, 1, 2)
+        quantize(0, 0, 1)
+        multiply(0, 0, 1)
+        exponentiate(1, 0, 1)
+        scale(0, 2, 3)
+        quantize(0, 1, 2)
+        multiply(0, 1, 2)
+        exponentiate(1, 1, 2)
+        quantize(0, 2, 3)
+        multiply(0, 2, 3)
+        scale(1, 0, 1)
+        exponentiate(1, 2, 3)
+        scale(1, 1, 2)
+        quantize(1, 0, 1)
+        multiply(1, 0, 1)
+        exponentiate(0, 3, 4)
+        scale(1, 2, 3)
+        quantize(1, 1, 2)
+        multiply(1, 1, 2)
+        drain(0, 0, "scalar")
+        scale(0, 3, 4)
+        quantize(1, 2, 3)
+        multiply(1, 2, 3)
+        drain(0, 1, "scalar")
+        exponentiate(1, 3, 4)
+        quantize(0, 3, 4)
+        multiply(0, 3, 4)
+        drain(1, 0, "vector")
+        scale(1, 3, 4)
+        drain(1, 1, "scalar")
+        drain(2, 0, "vector")
+        quantize(1, 3, 4)
+        multiply(1, 3, 4)
+        drain(2, 1, "scalar")
+        drain(3, 0, "vector")
+        drain(3, 1, "scalar")

@@ -32,140 +32,148 @@ def tile_mix_kvmix_tm_none_kernel(tc, lg, vs, v4_words, v4_scales, v8_words, v8_
         psum = ctx.enter_context(tc.psum_pool(name="psum", bufs=1))
         ctx.enter_context(tc.manual_schedule())
 
+        units = [(h, j) for h in range(2) for j in range(j_tiles)]
         warm = keep.tile([P, 1], F32, name="warm")
         warmed = keep.tile([P, 1], F32, name="warmed")
         vs_sb = keep.tile([P, 2, PACK], F32, name="vs_sb")
-        logits = [keep.tile([P, PACK, J], F32, name="logits%d" % h) for h in range(2)]
-        exps = [keep.tile([P, PACK, J], F32, name="exps%d" % h) for h in range(2)]
-        grouped = [keep.tile([P, J * PACK], BF16, name="grouped%d" % h, align_bytes=64) for h in range(2)]
-        e_codes = [keep.tile([P, J], U32, name="e_codes%d" % h, align_bytes=64) for h in range(2)]
-        e_scales = [keep.tile([P, J], U8, name="e_scales%d" % h, align_bytes=64) for h in range(2)]
-        v4_sb = keep.tile([P, 2 * D], U8, name="v4_sb", align_bytes=64)
-        v8_sb = keep.tile([P, D], U32, name="v8_sb", align_bytes=64)
+        logits = {}
+        exps = {u: keep.tile([P, PACK, J_TILE], F32, name="exps%d_%d" % u) for u in units}
+        grouped = {u: keep.tile([P, J_TILE * PACK], BF16, name="grouped%d_%d" % u, align_bytes=64) for u in units}
+        e_codes = {u: keep.tile([P, J_TILE], U32, name="e_codes%d_%d" % u, align_bytes=64) for u in units}
+        e_scales = {u: keep.tile([P, J_TILE], U8, name="e_scales%d_%d" % u, align_bytes=64) for u in units}
+        v_codes = {}
         v_scales = [keep.tile([P, D], U8, name="v_scales%d" % h, align_bytes=64) for h in range(2)]
-        results = [keep.tile([P, D], F32, name="results%d" % j) for j in range(j_tiles)]
+        results = [[keep.tile([P, N_TILE], F32, name="results%d_%d" % (j, n)) for n in range(n_tiles)] for j in range(j_tiles)]
         accs = [
             [psum.tile([P, N_TILE], F32, name="acc%d_%d" % (j, n)) for n in range(n_tiles)] for j in range(j_tiles)
         ]
+        opened = set()
 
-        def load_logits(h, j0, j1):
-            rows = lg[h * HALF : (h + 1) * HALF, j0:j1].rearrange("(p i) j -> p i j", i=PACK)
-            nc.sync.dma_start(out=logits[h][:, :, j0:j1], in_=rows)
+        def load_logits(h, j0, j1, engine=nc.sync):
+            chunk = keep.tile([P, PACK, (j1 - j0) * J_TILE], F32, name="logits%d_%d" % (h, j0))
+            rows = lg[h * HALF : (h + 1) * HALF, j0 * J_TILE : j1 * J_TILE].rearrange("(p i) j -> p i j", i=PACK)
+            engine.dma_start(out=chunk[:], in_=rows)
+            for j in range(j0, j1):
+                logits[(h, j)] = chunk[:, :, (j - j0) * J_TILE : (j - j0 + 1) * J_TILE]
 
-        def load_scales(engine, h, scales):
-            for q in range(4):
+        def load_scales(engine, h, q0=0, q1=4):
+            scales = (v4_scales, v8_scales)[h]
+            for q in range(q0, q1):
                 engine.dma_start(
                     out=v_scales[h][32 * q : 32 * q + 4, :].bitcast(I32),
                     in_=scales[0, 4 * q : 4 * q + 4, :].bitcast(I32),
                 )
 
-        nc.vector.memset(warm[:], 0.0)
-        nc.vector.memset(v_scales[0][:].bitcast(I32), 0)
-        nc.vector.memset(v_scales[1][:].bitcast(I32), 0)
-        def load_v8(n):
-            cols = slice(n * N_TILE, (n + 1) * N_TILE)
-            nc.sync.dma_start(
-                out=v8_sb[:, cols].bitcast(I32),
-                in_=v8_words[0].rearrange("p n t -> p (n t)")[:, 4 * n * N_TILE : 4 * (n + 1) * N_TILE].bitcast(I32),
-            )
+        def load_v(h, n0, n1, engine=nc.sync):
+            per = (2, 4)[h] * N_TILE
+            words = v4_words[0] if h == 0 else v8_words[0].rearrange("p n t -> p (n t)")
+            chunk = keep.tile([P, (n1 - n0) * per], U8, name="v%d_%d" % (h, n0), align_bytes=64)
+            engine.dma_start(out=chunk[:].bitcast(I32), in_=words[:, n0 * per : n1 * per].bitcast(I32))
+            for n in range(n0, n1):
+                v_codes[(h, n)] = chunk[:, (n - n0) * per : (n - n0 + 1) * per].bitcast((FP4X4, FP8X4)[h])
 
-        nc.scalar.dma_start(out=vs_sb[:], in_=vs.rearrange("(h p i) -> p h i", h=2, i=PACK))
-        load_logits(0, 0, 384)
-        load_scales(nc.scalar, 0, v4_scales)
-        nc.scalar.activation(out=warmed[:], in_=warm[:], func=EXP)
-        load_logits(1, 0, 384)
-        nc.sync.dma_start(out=v4_sb[:].bitcast(I32), in_=v4_words[0].bitcast(I32))
-        load_scales(nc.sync, 1, v8_scales)
-        load_logits(0, 384, 512)
-        load_v8(0)
-        load_v8(1)
-        load_logits(1, 384, 512)
+        def load_vs(engine):
+            engine.dma_start(out=vs_sb[:], in_=vs.rearrange("(h p i) -> p h i", h=2, i=PACK))
 
-        def cols(j0, j1, per=1):
-            return slice(per * j0 * J_TILE, per * j1 * J_TILE)
+        def exponentiate(h, j):
+            nc.scalar.activation(out=exps[(h, j)][:], in_=logits[(h, j)], func=EXP)
 
-        def exponentiate(h, j0, j1):
-            nc.scalar.activation(out=exps[h][:, :, cols(j0, j1)], in_=logits[h][:, :, cols(j0, j1)], func=EXP)
-
-        def scale(h, j0, j1):
-            pairs = (j1 - j0) * J_TILE // 2
+        def scale(h, j):
+            pairs = J_TILE // 2
             factor = vs_sb[:, h, :].unsqueeze(1).unsqueeze(3).to_broadcast([P, pairs, PACK, 2])
             nc.vector.tensor_tensor(
-                out=grouped[h][:, cols(j0, j1, PACK)].rearrange("p (c u i) -> p c i u", u=2, i=PACK),
-                in0=exps[h][:, :, cols(j0, j1)].rearrange("p i (c u) -> p c i u", u=2),
+                out=grouped[(h, j)][:].rearrange("p (c u i) -> p c i u", u=2, i=PACK),
+                in0=exps[(h, j)][:].rearrange("p i (c u) -> p c i u", u=2),
                 in1=factor,
                 op=MULT,
             )
 
-        def quantize(h, j0, j1):
+        def quantize(h, j):
             nc.vector.quantize_mx(
-                out=e_codes[h][:, cols(j0, j1)].bitcast(FP8X4),
-                scales=e_scales[h][:, cols(j0, j1)],
-                in_=grouped[h][:, cols(j0, j1, PACK)],
+                out=e_codes[(h, j)][:].bitcast(FP8X4),
+                scales=e_scales[(h, j)][:],
+                in_=grouped[(h, j)][:],
             )
 
-        def multiply(h, j0, j1):
-            for j in range(j0, j1):
-                for n in range(n_tiles):
-                    if h == 0:
-                        moving = v4_sb[:, 2 * n * N_TILE : 2 * (n + 1) * N_TILE].bitcast(FP4X4)
-                    else:
-                        moving = v8_sb[:, n * N_TILE : (n + 1) * N_TILE].bitcast(FP8X4)
-                    nc.tensor.matmul_mx(
-                        out=accs[j][n][:],
-                        lhsT=e_codes[h][:, cols(j, j + 1)].bitcast(FP8X4),
-                        lhsT_scale=e_scales[h][:, cols(j, j + 1)],
-                        rhs=moving,
-                        rhs_scale=v_scales[h][:, n * N_TILE : (n + 1) * N_TILE],
-                        start=(h == 0),
-                        stop=(h == 1),
-                    )
+        def multiply(h, j, n):
+            first = (j, n) not in opened
+            opened.add((j, n))
+            nc.tensor.matmul_mx(
+                out=accs[j][n][:],
+                lhsT=e_codes[(h, j)][:].bitcast(FP8X4),
+                lhsT_scale=e_scales[(h, j)][:],
+                rhs=v_codes[(h, n)],
+                rhs_scale=v_scales[h][:, n * N_TILE : (n + 1) * N_TILE],
+                start=first,
+                stop=not first,
+            )
 
         def drain(j, n, engine):
-            d_cols = slice(n * N_TILE, (n + 1) * N_TILE)
             if engine == "scalar":
-                nc.scalar.copy(out=results[j][:, d_cols], in_=accs[j][n][:])
+                nc.scalar.copy(out=results[j][n][:], in_=accs[j][n][:])
             else:
-                nc.vector.tensor_copy(out=results[j][:, d_cols], in_=accs[j][n][:])
-            nc.sync.dma_start(out=out[j * J_TILE : (j + 1) * J_TILE, d_cols], in_=results[j][:, d_cols])
+                nc.vector.tensor_copy(out=results[j][n][:], in_=accs[j][n][:])
+            nc.sync.dma_start(out=out[j * J_TILE : (j + 1) * J_TILE, n * N_TILE : (n + 1) * N_TILE], in_=results[j][n][:])
 
-        exponentiate(0, 0, 1)
-        exponentiate(0, 1, 2)
-        scale(0, 0, 1)
-        exponentiate(0, 2, 3)
-        scale(0, 1, 2)
-        quantize(0, 0, 1)
+        nc.vector.memset(warm[:], 0.0)
+        nc.vector.memset(v_scales[0][:].bitcast(I32), 0)
+        nc.vector.memset(v_scales[1][:].bitcast(I32), 0)
+        load_logits(0, 0, 3)
+        load_vs(nc.scalar)
+        nc.scalar.activation(out=warmed[:], in_=warm[:], func=EXP)
+        load_scales(nc.scalar, 0, 0, 4)
+        load_logits(1, 0, 3)
+        load_v(0, 0, 2)
+        load_logits(0, 3, 4)
+        load_v(1, 0, 1)
+        exponentiate(0, 0)
+        exponentiate(0, 1)
+        scale(0, 0)
+        exponentiate(0, 2)
+        load_scales(nc.scalar, 1, 0, 4)
+        load_v(1, 1, 2)
+        load_logits(1, 3, 4)
+        scale(0, 1)
+        quantize(0, 0)
+        scale(0, 2)
+        quantize(0, 1)
+        exponentiate(1, 0)
+        quantize(0, 2)
+        exponentiate(1, 1)
+        scale(1, 0)
+        exponentiate(1, 2)
+        scale(1, 1)
+        quantize(1, 0)
+        multiply(0, 0, 0)
+        multiply(0, 1, 0)
         multiply(0, 0, 1)
-        exponentiate(1, 0, 1)
-        scale(0, 2, 3)
-        quantize(0, 1, 2)
-        multiply(0, 1, 2)
-        exponentiate(1, 1, 2)
-        quantize(0, 2, 3)
-        multiply(0, 2, 3)
-        scale(1, 0, 1)
-        exponentiate(1, 2, 3)
-        scale(1, 1, 2)
-        quantize(1, 0, 1)
+        multiply(1, 0, 0)
+        exponentiate(0, 3)
+        scale(1, 2)
+        quantize(1, 1)
+        multiply(1, 1, 0)
+        multiply(0, 1, 1)
         multiply(1, 0, 1)
-        exponentiate(0, 3, 4)
-        scale(1, 2, 3)
-        quantize(1, 1, 2)
-        multiply(1, 1, 2)
+        multiply(1, 1, 1)
         drain(0, 0, "scalar")
-        scale(0, 3, 4)
-        quantize(1, 2, 3)
-        multiply(1, 2, 3)
-        drain(0, 1, "scalar")
-        exponentiate(1, 3, 4)
-        quantize(0, 3, 4)
-        multiply(0, 3, 4)
-        drain(1, 0, "vector")
-        scale(1, 3, 4)
+        scale(0, 3)
+        quantize(1, 2)
+        multiply(0, 2, 0)
+        multiply(1, 2, 0)
+        multiply(0, 2, 1)
+        multiply(1, 2, 1)
+        drain(1, 0, "scalar")
+        exponentiate(1, 3)
+        drain(0, 1, "vector")
+        quantize(0, 3)
+        multiply(0, 3, 0)
+        multiply(0, 3, 1)
         drain(1, 1, "scalar")
-        drain(2, 0, "vector")
-        quantize(1, 3, 4)
-        multiply(1, 3, 4)
-        drain(2, 1, "scalar")
-        drain(3, 0, "vector")
-        drain(3, 1, "scalar")
+        scale(1, 3)
+        drain(2, 0, "scalar")
+        quantize(1, 3)
+        multiply(1, 3, 0)
+        multiply(1, 3, 1)
+        drain(2, 1, "vector")
+        drain(3, 0, "scalar")
+        drain(3, 1, "vector")

@@ -37,7 +37,7 @@ def tile_mix_kvmix_tm_none_kernel(tc, lg, vs, v4_words, v4_scales, v8_words, v8_
         warmed = keep.tile([P, 1], F32, name="warmed")
         vs_sb = keep.tile([P, 2, PACK], F32, name="vs_sb")
         logits = {}
-        exps = {u: keep.tile([P, PACK, J_TILE], F32, name="exps%d_%d" % u) for u in units}
+        exps = {u: keep.tile([P, 2, J_TILE, 2], F32, name="exps%d_%d" % u) for u in units}
         grouped = {u: keep.tile([P, J_TILE * PACK], BF16, name="grouped%d_%d" % u, align_bytes=64) for u in units}
         e_codes = {u: keep.tile([P, J_TILE], U32, name="e_codes%d_%d" % u, align_bytes=64) for u in units}
         e_scales = {u: keep.tile([P, J_TILE], U8, name="e_scales%d_%d" % u, align_bytes=64) for u in units}
@@ -76,14 +76,13 @@ def tile_mix_kvmix_tm_none_kernel(tc, lg, vs, v4_words, v4_scales, v8_words, v8_
             engine.dma_start(out=vs_sb[:], in_=vs.rearrange("(h p i) -> p h i", h=2, i=PACK))
 
         def exponentiate(h, j):
-            nc.scalar.activation(out=exps[(h, j)][:], in_=logits[(h, j)], func=EXP)
+            nc.scalar.activation(out=exps[(h, j)][:], in_=logits[(h, j)].rearrange("p (a b) c -> p a c b", b=2), func=EXP)
 
         def scale(h, j):
-            pairs = J_TILE // 2
-            factor = vs_sb[:, h, :].unsqueeze(1).unsqueeze(3).to_broadcast([P, pairs, PACK, 2])
+            factor = vs_sb[:, h, :].rearrange("p (a b) -> p a b", b=2).unsqueeze(1).to_broadcast([P, J_TILE, 2, 2])
             nc.vector.tensor_tensor(
-                out=grouped[(h, j)][:].rearrange("p (c u i) -> p c i u", u=2, i=PACK),
-                in0=exps[(h, j)][:].rearrange("p i (c u) -> p c i u", u=2),
+                out=grouped[(h, j)][:].rearrange("p (c a b) -> p c a b", a=2, b=2),
+                in0=exps[(h, j)][:].rearrange("p a c b -> p c a b"),
                 in1=factor,
                 op=MULT,
             )
@@ -118,21 +117,21 @@ def tile_mix_kvmix_tm_none_kernel(tc, lg, vs, v4_words, v4_scales, v8_words, v8_
         nc.vector.memset(warm[:], 0.0)
         nc.vector.memset(v_scales[0][:].bitcast(I32), 0)
         nc.vector.memset(v_scales[1][:].bitcast(I32), 0)
-        load_logits(0, 0, 3)
         load_vs(nc.scalar)
-        nc.scalar.activation(out=warmed[:], in_=warm[:], func=EXP)
+        load_logits(0, 0, 3)
         load_scales(nc.scalar, 0, 0, 4)
+        nc.scalar.activation(out=warmed[:], in_=warm[:], func=EXP)
         load_logits(1, 0, 3)
         load_v(0, 0, 2)
+        load_scales(nc.sync, 1, 0, 4)
         load_logits(0, 3, 4)
         load_v(1, 0, 1)
+        load_v(1, 1, 2)
+        load_logits(1, 3, 4)
         exponentiate(0, 0)
         exponentiate(0, 1)
         scale(0, 0)
         exponentiate(0, 2)
-        load_scales(nc.scalar, 1, 0, 4)
-        load_v(1, 1, 2)
-        load_logits(1, 3, 4)
         scale(0, 1)
         quantize(0, 0)
         scale(0, 2)

@@ -75,14 +75,14 @@ def tile_mix_kvmix_tm_none_kernel(tc, lg, vs, v4_words, v4_scales, v8_words, v8_
         def load_vs(engine):
             engine.dma_start(out=vs_sb[:], in_=vs.rearrange("(h p i) -> p h i", h=2, i=PACK))
 
-        def exponentiate(h, j):
-            nc.scalar.activation(out=exps[(h, j)][:], in_=logits[(h, j)].rearrange("p (a b) c -> p a c b", b=2), func=EXP)
+        def exponentiate(h, j, c0=0, c1=J_TILE):
+            nc.scalar.activation(out=exps[(h, j)][:, :, c0:c1, :], in_=logits[(h, j)][:, :, c0:c1].rearrange("p (a b) c -> p a c b", b=2), func=EXP)
 
-        def scale(h, j):
-            factor = vs_sb[:, h, :].rearrange("p (a b) -> p a b", b=2).unsqueeze(1).to_broadcast([P, J_TILE, 2, 2])
+        def scale(h, j, c0=0, c1=J_TILE):
+            factor = vs_sb[:, h, :].rearrange("p (a b) -> p a b", b=2).unsqueeze(1).to_broadcast([P, c1 - c0, 2, 2])
             nc.vector.tensor_tensor(
-                out=grouped[(h, j)][:].rearrange("p (c a b) -> p c a b", a=2, b=2),
-                in0=exps[(h, j)][:].rearrange("p a c b -> p c a b"),
+                out=grouped[(h, j)][:, PACK * c0 : PACK * c1].rearrange("p (c a b) -> p c a b", a=2, b=2),
+                in0=exps[(h, j)][:, :, c0:c1, :].rearrange("p a c b -> p c a b"),
                 in1=factor,
                 op=MULT,
             )
@@ -107,26 +107,28 @@ def tile_mix_kvmix_tm_none_kernel(tc, lg, vs, v4_words, v4_scales, v8_words, v8_
                 stop=not first,
             )
 
-        def drain(j, n, engine):
+        def drain(j, n, engine, c0=0, c1=N_TILE):
             if engine == "scalar":
-                nc.scalar.copy(out=results[j][n][:], in_=accs[j][n][:])
+                nc.scalar.copy(out=results[j][n][:, c0:c1], in_=accs[j][n][:, c0:c1])
             else:
-                nc.vector.tensor_copy(out=results[j][n][:], in_=accs[j][n][:])
-            nc.sync.dma_start(out=out[j * J_TILE : (j + 1) * J_TILE, n * N_TILE : (n + 1) * N_TILE], in_=results[j][n][:])
+                nc.vector.tensor_copy(out=results[j][n][:, c0:c1], in_=accs[j][n][:, c0:c1])
+            nc.sync.dma_start(
+                out=out[j * J_TILE : (j + 1) * J_TILE, n * N_TILE + c0 : n * N_TILE + c1], in_=results[j][n][:, c0:c1]
+            )
 
         nc.vector.memset(warm[:], 0.0)
         nc.vector.memset(v_scales[0][:].bitcast(I32), 0)
         nc.vector.memset(v_scales[1][:].bitcast(I32), 0)
-        load_vs(nc.scalar)
         load_logits(0, 0, 3)
-        load_scales(nc.scalar, 0, 0, 4)
         nc.scalar.activation(out=warmed[:], in_=warm[:], func=EXP)
+        load_vs(nc.sync)
         load_logits(1, 0, 3)
+        load_scales(nc.sync, 0, 0, 4)
         load_v(0, 0, 2)
-        load_scales(nc.sync, 1, 0, 4)
-        load_logits(0, 3, 4)
         load_v(1, 0, 1)
+        load_scales(nc.sync, 1, 0, 4)
         load_v(1, 1, 2)
+        load_logits(0, 3, 4)
         load_logits(1, 3, 4)
         exponentiate(0, 0)
         exponentiate(0, 1)
@@ -137,42 +139,42 @@ def tile_mix_kvmix_tm_none_kernel(tc, lg, vs, v4_words, v4_scales, v8_words, v8_
         scale(0, 2)
         quantize(0, 1)
         exponentiate(1, 0)
-        quantize(0, 2)
         exponentiate(1, 1)
         scale(1, 0)
-        exponentiate(1, 2)
-        scale(1, 1)
+        quantize(0, 2)
         quantize(1, 0)
         multiply(0, 0, 0)
-        multiply(0, 1, 0)
         multiply(0, 0, 1)
         multiply(1, 0, 0)
-        exponentiate(0, 3)
+        multiply(1, 0, 1)
+        multiply(0, 1, 0)
+        multiply(0, 1, 1)
+        exponentiate(1, 2)
+        scale(1, 1)
+        drain(0, 0, "scalar")
         scale(1, 2)
         quantize(1, 1)
         multiply(1, 1, 0)
-        multiply(0, 1, 1)
-        multiply(1, 0, 1)
         multiply(1, 1, 1)
-        drain(0, 0, "scalar")
-        scale(0, 3)
         quantize(1, 2)
         multiply(0, 2, 0)
         multiply(1, 2, 0)
         multiply(0, 2, 1)
         multiply(1, 2, 1)
-        drain(1, 0, "scalar")
-        exponentiate(1, 3)
+        exponentiate(0, 3)
         drain(0, 1, "vector")
-        quantize(0, 3)
-        multiply(0, 3, 0)
-        multiply(0, 3, 1)
-        drain(1, 1, "scalar")
+        exponentiate(1, 3)
+        scale(0, 3)
+        drain(1, 0, "scalar")
         scale(1, 3)
-        drain(2, 0, "scalar")
+        quantize(0, 3)
+        drain(1, 1, "scalar")
         quantize(1, 3)
+        multiply(0, 3, 0)
         multiply(1, 3, 0)
+        multiply(0, 3, 1)
         multiply(1, 3, 1)
-        drain(2, 1, "vector")
-        drain(3, 0, "scalar")
-        drain(3, 1, "vector")
+        drain(2, 0, "vector")
+        drain(2, 1, "scalar")
+        drain(3, 0, "vector")
+        drain(3, 1, "scalar")

@@ -37,7 +37,8 @@ def tile_mix_kvmix_tm_none_kernel(tc, lg, vs, v4_words, v4_scales, v8_words, v8_
         warmed = keep.tile([P, 1], F32, name="warmed")
         vs_sb = keep.tile([P, 2, PACK], F32, name="vs_sb")
         logits = {}
-        exps = {u: keep.tile([P, 2, J_TILE, 2], F32, name="exps%d_%d" % u) for u in units}
+        exps = {}
+        halves = {}
         grouped = {u: keep.tile([P, J_TILE * PACK], BF16, name="grouped%d_%d" % u, align_bytes=64) for u in units}
         e_codes = {u: keep.tile([P, J_TILE], U32, name="e_codes%d_%d" % u, align_bytes=64) for u in units}
         e_scales = {u: keep.tile([P, J_TILE], U8, name="e_scales%d_%d" % u, align_bytes=64) for u in units}
@@ -53,15 +54,34 @@ def tile_mix_kvmix_tm_none_kernel(tc, lg, vs, v4_words, v4_scales, v8_words, v8_
             chunk = keep.tile([P, PACK, (j1 - j0) * J_TILE], F32, name="logits%d_%d" % (h, j0))
             rows = lg[h * HALF : (h + 1) * HALF, j0 * J_TILE : j1 * J_TILE].rearrange("(p i) j -> p i j", i=PACK)
             engine.dma_start(out=chunk[:], in_=rows)
+            paired = keep.tile([P, 2, (j1 - j0) * J_TILE, 2], F32, name="exps%d_%d" % (h, j0))
             for j in range(j0, j1):
                 logits[(h, j)] = chunk[:, :, (j - j0) * J_TILE : (j - j0 + 1) * J_TILE]
+                exps[(h, j)] = paired[:, :, (j - j0) * J_TILE : (j - j0 + 1) * J_TILE, :]
+
+        def load_pair(h, a, j0, j1):
+            chunk = keep.tile([P, 2, (j1 - j0) * J_TILE], F32, name="pair%d_%d_%d" % (h, a, j0))
+            rows = lg[h * HALF : (h + 1) * HALF, j0 * J_TILE : j1 * J_TILE].rearrange("(p i) j -> p i j", i=PACK)
+            nc.sync.dma_start(out=chunk[:], in_=rows[:, 2 * a : 2 * a + 2, :])
+            if a == 0:
+                paired = keep.tile([P, 2, (j1 - j0) * J_TILE, 2], F32, name="exps%d_%d" % (h, j0))
+                halves[(h, j0)] = (chunk, paired)
+                for j in range(j0, j1):
+                    exps[(h, j)] = paired[:, :, (j - j0) * J_TILE : (j - j0 + 1) * J_TILE, :]
+            else:
+                for j in range(j0, j1):
+                    halves[(h, j, 1)] = chunk[:, :, (j - j0) * J_TILE : (j - j0 + 1) * J_TILE]
+
+        def exponentiate_first_pair(h, j0):
+            chunk, paired = halves[(h, j0)]
+            nc.scalar.activation(out=paired[:, 0, :, :], in_=chunk[:].rearrange("p b c -> p c b"), func=EXP)
 
         def load_scales(engine, h, q0=0, q1=4):
             scales = (v4_scales, v8_scales)[h]
             for q in range(q0, q1):
                 engine.dma_start(
-                    out=v_scales[h][32 * q : 32 * q + 4, :].bitcast(I32),
-                    in_=scales[0, 4 * q : 4 * q + 4, :].bitcast(I32),
+                    out=v_scales[h][4 * h + q : P : 32, :].bitcast(I32),
+                    in_=scales[0, q:16:4, :].bitcast(I32),
                 )
 
         def load_v(h, n0, n1, engine=nc.sync):
@@ -75,8 +95,11 @@ def tile_mix_kvmix_tm_none_kernel(tc, lg, vs, v4_words, v4_scales, v8_words, v8_
         def load_vs(engine):
             engine.dma_start(out=vs_sb[:], in_=vs.rearrange("(h p i) -> p h i", h=2, i=PACK))
 
-        def exponentiate(h, j, c0=0, c1=J_TILE):
-            nc.scalar.activation(out=exps[(h, j)][:, :, c0:c1, :], in_=logits[(h, j)][:, :, c0:c1].rearrange("p (a b) c -> p a c b", b=2), func=EXP)
+        def exponentiate(h, j):
+            if (h, j, 1) in halves:
+                nc.scalar.activation(out=exps[(h, j)][:, 1, :, :], in_=halves[(h, j, 1)].rearrange("p b c -> p c b"), func=EXP)
+            else:
+                nc.scalar.activation(out=exps[(h, j)], in_=logits[(h, j)].rearrange("p (a b) c -> p a c b", b=2), func=EXP)
 
         def scale(h, j, c0=0, c1=J_TILE):
             factor = vs_sb[:, h, :].rearrange("p (a b) -> p a b", b=2).unsqueeze(1).to_broadcast([P, c1 - c0, 2, 2])
@@ -102,7 +125,7 @@ def tile_mix_kvmix_tm_none_kernel(tc, lg, vs, v4_words, v4_scales, v8_words, v8_
                 lhsT=e_codes[(h, j)][:].bitcast(FP8X4),
                 lhsT_scale=e_scales[(h, j)][:],
                 rhs=v_codes[(h, n)],
-                rhs_scale=v_scales[h][:, n * N_TILE : (n + 1) * N_TILE],
+                rhs_scale=v_scales[h][4 * h :, n * N_TILE : (n + 1) * N_TILE],
                 start=first,
                 stop=not first,
             )
@@ -119,17 +142,21 @@ def tile_mix_kvmix_tm_none_kernel(tc, lg, vs, v4_words, v4_scales, v8_words, v8_
         nc.vector.memset(warm[:], 0.0)
         nc.vector.memset(v_scales[0][:].bitcast(I32), 0)
         nc.vector.memset(v_scales[1][:].bitcast(I32), 0)
-        load_logits(0, 0, 3)
+        load_pair(0, 0, 0, 3)
+        load_pair(0, 1, 0, 3)
         nc.scalar.activation(out=warmed[:], in_=warm[:], func=EXP)
         load_vs(nc.sync)
-        load_logits(1, 0, 3)
+        load_pair(1, 0, 0, 3)
+        load_pair(1, 1, 0, 3)
         load_scales(nc.sync, 0, 0, 4)
         load_v(0, 0, 2)
+        load_logits(0, 3, 4)
         load_v(1, 0, 1)
         load_scales(nc.sync, 1, 0, 4)
         load_v(1, 1, 2)
-        load_logits(0, 3, 4)
-        load_logits(1, 3, 4)
+        load_pair(1, 0, 3, 4)
+        load_pair(1, 1, 3, 4)
+        exponentiate_first_pair(0, 0)
         exponentiate(0, 0)
         exponentiate(0, 1)
         scale(0, 0)
@@ -138,43 +165,45 @@ def tile_mix_kvmix_tm_none_kernel(tc, lg, vs, v4_words, v4_scales, v8_words, v8_
         quantize(0, 0)
         scale(0, 2)
         quantize(0, 1)
+        exponentiate_first_pair(1, 0)
         exponentiate(1, 0)
         exponentiate(1, 1)
         scale(1, 0)
         quantize(0, 2)
+        exponentiate(1, 2)
         quantize(1, 0)
+        scale(1, 1)
         multiply(0, 0, 0)
         multiply(0, 0, 1)
-        multiply(1, 0, 0)
-        multiply(1, 0, 1)
         multiply(0, 1, 0)
-        multiply(0, 1, 1)
-        exponentiate(1, 2)
-        scale(1, 1)
-        drain(0, 0, "scalar")
+        multiply(1, 0, 0)
+        exponentiate(0, 3)
         scale(1, 2)
         quantize(1, 1)
+        multiply(1, 0, 1)
         multiply(1, 1, 0)
+        multiply(0, 1, 1)
         multiply(1, 1, 1)
+        scale(0, 3)
         quantize(1, 2)
         multiply(0, 2, 0)
         multiply(1, 2, 0)
         multiply(0, 2, 1)
         multiply(1, 2, 1)
-        exponentiate(0, 3)
+        drain(0, 0, "scalar")
+        exponentiate_first_pair(1, 3)
         drain(0, 1, "vector")
-        exponentiate(1, 3)
-        scale(0, 3)
-        drain(1, 0, "scalar")
-        scale(1, 3)
         quantize(0, 3)
-        drain(1, 1, "scalar")
-        quantize(1, 3)
+        exponentiate(1, 3)
+        drain(1, 0, "scalar")
         multiply(0, 3, 0)
-        multiply(1, 3, 0)
         multiply(0, 3, 1)
-        multiply(1, 3, 1)
+        scale(1, 3)
+        quantize(1, 3)
+        drain(1, 1, "scalar")
         drain(2, 0, "vector")
+        multiply(1, 3, 0)
+        multiply(1, 3, 1)
         drain(2, 1, "scalar")
         drain(3, 0, "vector")
         drain(3, 1, "scalar")

@@ -141,7 +141,8 @@ def tile_mix_kvmix_tm_none_kernel(tc, lg, vs, v4_words, v4_scales, v8_words, v8_
 
         nc.vector.memset(warm[:], 0.0)
         nc.vector.memset(v_scales[0][:].bitcast(I32), 0)
-        nc.vector.memset(v_scales[1][:].bitcast(I32), 0)
+        nc.gpsimd.memset(v_scales[1][:].bitcast(I32), 0)
+        load_scales(nc.gpsimd, 1, 0, 4)
         load_pair(0, 0, 0, 3)
         load_pair(0, 1, 0, 3)
         nc.scalar.activation(out=warmed[:], in_=warm[:], func=EXP)
@@ -152,7 +153,6 @@ def tile_mix_kvmix_tm_none_kernel(tc, lg, vs, v4_words, v4_scales, v8_words, v8_
         load_v(0, 0, 2)
         load_logits(0, 3, 4)
         load_v(1, 0, 1)
-        load_scales(nc.sync, 1, 0, 4)
         load_v(1, 1, 2)
         load_pair(1, 0, 3, 4)
         load_pair(1, 1, 3, 4)

@@ -33,48 +33,39 @@ def tile_mix_kvmix_tm_none_kernel(tc, lg, vs, v4_words, v4_scales, v8_words, v8_
         ctx.enter_context(tc.manual_schedule())
 
         units = [(h, j) for h in range(2) for j in range(j_tiles)]
-        warm = keep.tile([P, 1], F32, name="warm")
-        warmed = keep.tile([P, 1], F32, name="warmed")
         vs_sb = keep.tile([P, 2, PACK], F32, name="vs_sb")
         logits = {}
         exps = {}
-        halves = {}
         grouped = {u: keep.tile([P, J_TILE * PACK], BF16, name="grouped%d_%d" % u, align_bytes=64) for u in units}
         e_codes = {u: keep.tile([P, J_TILE], U32, name="e_codes%d_%d" % u, align_bytes=64) for u in units}
         e_scales = {u: keep.tile([P, J_TILE], U8, name="e_scales%d_%d" % u, align_bytes=64) for u in units}
         v_codes = {}
         v_scales = [keep.tile([P, D], U8, name="v_scales%d" % h, align_bytes=64) for h in range(2)]
-        results = [[keep.tile([P, N_TILE], F32, name="results%d_%d" % (j, n)) for n in range(n_tiles)] for j in range(j_tiles)]
+        results = [keep.tile([P, D], F32, name="results%d" % j) for j in range(j_tiles)]
         accs = [
             [psum.tile([P, N_TILE], F32, name="acc%d_%d" % (j, n)) for n in range(n_tiles)] for j in range(j_tiles)
         ]
         opened = set()
 
-        def load_logits(h, j0, j1, engine=nc.sync):
-            chunk = keep.tile([P, PACK, (j1 - j0) * J_TILE], F32, name="logits%d_%d" % (h, j0))
+        def load_lg(h, j0, j1, a0=0, a1=2, engine=nc.sync):
+            width = (j1 - j0) * J_TILE
+            chunk = keep.tile([P, 2 * (a1 - a0), width], F32, name="lg%d_%d_%d" % (h, j0, a0))
             rows = lg[h * HALF : (h + 1) * HALF, j0 * J_TILE : j1 * J_TILE].rearrange("(p i) j -> p i j", i=PACK)
-            engine.dma_start(out=chunk[:], in_=rows)
-            paired = keep.tile([P, 2, (j1 - j0) * J_TILE, 2], F32, name="exps%d_%d" % (h, j0))
+            engine.dma_start(out=chunk[:], in_=rows[:, 2 * a0 : 2 * a1, :])
+            if (h, j0) not in exps:
+                paired = keep.tile([P, 2, width, 2], F32, name="exps%d_%d" % (h, j0))
+                for j in range(j0, j1):
+                    exps[(h, j)] = (paired, j0)
             for j in range(j0, j1):
-                logits[(h, j)] = chunk[:, :, (j - j0) * J_TILE : (j - j0 + 1) * J_TILE]
-                exps[(h, j)] = paired[:, :, (j - j0) * J_TILE : (j - j0 + 1) * J_TILE, :]
+                for a in range(a0, a1):
+                    logits[(h, j, a)] = (chunk, j0, a0)
 
-        def load_pair(h, a, j0, j1):
-            chunk = keep.tile([P, 2, (j1 - j0) * J_TILE], F32, name="pair%d_%d_%d" % (h, a, j0))
-            rows = lg[h * HALF : (h + 1) * HALF, j0 * J_TILE : j1 * J_TILE].rearrange("(p i) j -> p i j", i=PACK)
-            nc.sync.dma_start(out=chunk[:], in_=rows[:, 2 * a : 2 * a + 2, :])
-            if a == 0:
-                paired = keep.tile([P, 2, (j1 - j0) * J_TILE, 2], F32, name="exps%d_%d" % (h, j0))
-                halves[(h, j0)] = (chunk, paired)
-                for j in range(j0, j1):
-                    exps[(h, j)] = paired[:, :, (j - j0) * J_TILE : (j - j0 + 1) * J_TILE, :]
-            else:
-                for j in range(j0, j1):
-                    halves[(h, j, 1)] = chunk[:, :, (j - j0) * J_TILE : (j - j0 + 1) * J_TILE]
-
-        def exponentiate_first_pair(h, j0):
-            chunk, paired = halves[(h, j0)]
-            nc.scalar.activation(out=paired[:, 0, :, :], in_=chunk[:].rearrange("p b c -> p c b"), func=EXP)
+        def exponentiate(h, j0, j1, a0=0, a1=2):
+            chunk, first_j, first_a = logits[(h, j0, a0)]
+            paired, paired_j = exps[(h, j0)]
+            src = chunk[:, 2 * (a0 - first_a) : 2 * (a1 - first_a), (j0 - first_j) * J_TILE : (j1 - first_j) * J_TILE]
+            dst = paired[:, a0:a1, (j0 - paired_j) * J_TILE : (j1 - paired_j) * J_TILE, :]
+            nc.scalar.activation(out=dst, in_=src.rearrange("p (a b) c -> p a c b", b=2), func=EXP)
 
         def load_scales(engine, h, q0=0, q1=4):
             scales = (v4_scales, v8_scales)[h]
@@ -95,17 +86,13 @@ def tile_mix_kvmix_tm_none_kernel(tc, lg, vs, v4_words, v4_scales, v8_words, v8_
         def load_vs(engine):
             engine.dma_start(out=vs_sb[:], in_=vs.rearrange("(h p i) -> p h i", h=2, i=PACK))
 
-        def exponentiate(h, j):
-            if (h, j, 1) in halves:
-                nc.scalar.activation(out=exps[(h, j)][:, 1, :, :], in_=halves[(h, j, 1)].rearrange("p b c -> p c b"), func=EXP)
-            else:
-                nc.scalar.activation(out=exps[(h, j)], in_=logits[(h, j)].rearrange("p (a b) c -> p a c b", b=2), func=EXP)
-
-        def scale(h, j, c0=0, c1=J_TILE):
+        def scale(h, j, engine=nc.vector, c0=0, c1=J_TILE):
+            paired, paired_j = exps[(h, j)]
+            base = (j - paired_j) * J_TILE
             factor = vs_sb[:, h, :].rearrange("p (a b) -> p a b", b=2).unsqueeze(1).to_broadcast([P, c1 - c0, 2, 2])
-            nc.vector.tensor_tensor(
+            engine.tensor_tensor(
                 out=grouped[(h, j)][:, PACK * c0 : PACK * c1].rearrange("p (c a b) -> p c a b", a=2, b=2),
-                in0=exps[(h, j)][:, :, c0:c1, :].rearrange("p a c b -> p c a b"),
+                in0=paired[:, :, base + c0 : base + c1, :].rearrange("p a c b -> p c a b"),
                 in1=factor,
                 op=MULT,
             )
@@ -130,80 +117,86 @@ def tile_mix_kvmix_tm_none_kernel(tc, lg, vs, v4_words, v4_scales, v8_words, v8_
                 stop=not first,
             )
 
-        def drain(j, n, engine, c0=0, c1=N_TILE):
+        def copy_out(j, n, engine, c0=0, c1=N_TILE):
+            dst = results[j][:, n * N_TILE + c0 : n * N_TILE + c1]
             if engine == "scalar":
-                nc.scalar.copy(out=results[j][n][:, c0:c1], in_=accs[j][n][:, c0:c1])
+                nc.scalar.copy(out=dst, in_=accs[j][n][:, c0:c1])
             else:
-                nc.vector.tensor_copy(out=results[j][n][:, c0:c1], in_=accs[j][n][:, c0:c1])
-            nc.sync.dma_start(
-                out=out[j * J_TILE : (j + 1) * J_TILE, n * N_TILE + c0 : n * N_TILE + c1], in_=results[j][n][:, c0:c1]
-            )
+                nc.vector.tensor_copy(out=dst, in_=accs[j][n][:, c0:c1])
 
-        nc.vector.memset(warm[:], 0.0)
+        def store(j, c0, c1, engine=nc.sync):
+            engine.dma_start(out=out[j * J_TILE : (j + 1) * J_TILE, c0:c1], in_=results[j][:, c0:c1])
+
+        def drain(j, n, engine):
+            copy_out(j, n, engine)
+            store(j, n * N_TILE, (n + 1) * N_TILE)
+
         nc.vector.memset(v_scales[0][:].bitcast(I32), 0)
         nc.gpsimd.memset(v_scales[1][:].bitcast(I32), 0)
         load_scales(nc.gpsimd, 1, 0, 4)
-        load_pair(0, 0, 0, 3)
-        load_pair(0, 1, 0, 3)
-        nc.scalar.activation(out=warmed[:], in_=warm[:], func=EXP)
+        load_lg(0, 0, 2, 0, 1)
+        load_lg(0, 0, 2, 1, 2)
         load_vs(nc.sync)
-        load_pair(1, 0, 0, 3)
-        load_pair(1, 1, 0, 3)
-        load_scales(nc.sync, 0, 0, 4)
+        load_lg(1, 0, 2, 0, 1)
+        load_lg(1, 0, 2, 1, 2)
+        load_scales(nc.sync, 0, 0, 2)
+        load_lg(0, 2, 4, 0, 1)
+        load_scales(nc.sync, 0, 2, 4)
         load_v(0, 0, 2)
-        load_logits(0, 3, 4)
+        load_lg(0, 2, 4, 1, 2)
+        load_lg(1, 2, 4, 0, 1)
         load_v(1, 0, 1)
+        load_lg(1, 2, 4, 1, 2)
         load_v(1, 1, 2)
-        load_pair(1, 0, 3, 4)
-        load_pair(1, 1, 3, 4)
-        exponentiate_first_pair(0, 0)
-        exponentiate(0, 0)
-        exponentiate(0, 1)
+        exponentiate(0, 0, 2, 0, 1)
+        exponentiate(0, 0, 1, 1, 2)
+        exponentiate(0, 1, 2, 1, 2)
         scale(0, 0)
-        exponentiate(0, 2)
+        exponentiate(1, 0, 2, 0, 1)
         scale(0, 1)
         quantize(0, 0)
-        scale(0, 2)
-        quantize(0, 1)
-        exponentiate_first_pair(1, 0)
-        exponentiate(1, 0)
-        exponentiate(1, 1)
+        exponentiate(1, 0, 1, 1, 2)
+        exponentiate(1, 1, 2, 1, 2)
         scale(1, 0)
-        quantize(0, 2)
-        exponentiate(1, 2)
-        quantize(1, 0)
+        quantize(0, 1)
+        exponentiate(0, 2, 4, 0, 1)
         scale(1, 1)
+        quantize(1, 0)
+        exponentiate(0, 2, 3, 1, 2)
+        exponentiate(0, 3, 4, 1, 2)
+        quantize(1, 1)
         multiply(0, 0, 0)
         multiply(0, 0, 1)
         multiply(0, 1, 0)
+        scale(0, 2)
         multiply(1, 0, 0)
-        exponentiate(0, 3)
-        scale(1, 2)
-        quantize(1, 1)
-        multiply(1, 0, 1)
         multiply(1, 1, 0)
-        multiply(0, 1, 1)
-        multiply(1, 1, 1)
+        exponentiate(1, 2, 4, 0, 1)
         scale(0, 3)
-        quantize(1, 2)
-        multiply(0, 2, 0)
-        multiply(1, 2, 0)
-        multiply(0, 2, 1)
-        multiply(1, 2, 1)
-        drain(0, 0, "scalar")
-        exponentiate_first_pair(1, 3)
-        drain(0, 1, "vector")
+        quantize(0, 2)
+        multiply(0, 1, 1)
+        drain(0, 0, "vector")
+        exponentiate(1, 2, 3, 1, 2)
+        exponentiate(1, 3, 4, 1, 2)
         quantize(0, 3)
-        exponentiate(1, 3)
+        multiply(0, 2, 0)
+        multiply(0, 2, 1)
         drain(1, 0, "scalar")
+        scale(1, 2)
+        multiply(1, 0, 1)
+        multiply(1, 1, 1)
         multiply(0, 3, 0)
         multiply(0, 3, 1)
+        drain(0, 1, "scalar")
         scale(1, 3)
-        quantize(1, 3)
+        quantize(1, 2)
+        multiply(1, 2, 0)
+        multiply(1, 2, 1)
         drain(1, 1, "scalar")
-        drain(2, 0, "vector")
+        quantize(1, 3)
         multiply(1, 3, 0)
         multiply(1, 3, 1)
+        drain(2, 0, "vector")
         drain(2, 1, "scalar")
         drain(3, 0, "vector")
         drain(3, 1, "scalar")

@@ -144,8 +144,8 @@ def tile_mix_kvmix_tm_none_kernel(tc, lg, vs, v4_words, v4_scales, v8_words, v8_
         load_scales(nc.sync, 0, 2, 4)
         load_v(0, 0, 2)
         load_lg(0, 2, 4, 1, 2)
-        load_lg(1, 2, 4, 0, 1)
         load_v(1, 0, 1)
+        load_lg(1, 2, 4, 0, 1)
         load_lg(1, 2, 4, 1, 2)
         load_v(1, 1, 2)
         exponentiate(0, 0, 2, 0, 1)
@@ -178,25 +178,25 @@ def tile_mix_kvmix_tm_none_kernel(tc, lg, vs, v4_words, v4_scales, v8_words, v8_
         drain(0, 0, "vector")
         exponentiate(1, 2, 3, 1, 2)
         exponentiate(1, 3, 4, 1, 2)
-        quantize(0, 3)
         multiply(0, 2, 0)
-        multiply(0, 2, 1)
         drain(1, 0, "scalar")
         scale(1, 2)
         multiply(1, 0, 1)
         multiply(1, 1, 1)
-        multiply(0, 3, 0)
-        multiply(0, 3, 1)
+        quantize(0, 3)
+        multiply(0, 2, 1)
         drain(0, 1, "scalar")
-        scale(1, 3)
         quantize(1, 2)
         multiply(1, 2, 0)
         multiply(1, 2, 1)
+        scale(1, 3)
+        multiply(0, 3, 0)
+        multiply(0, 3, 1)
         drain(1, 1, "scalar")
         quantize(1, 3)
         multiply(1, 3, 0)
         multiply(1, 3, 1)
-        drain(2, 0, "vector")
-        drain(2, 1, "scalar")
+        drain(2, 0, "scalar")
+        drain(2, 1, "vector")
         drain(3, 0, "vector")
         drain(3, 1, "scalar")

@@ -33,7 +33,7 @@ def tile_mix_kvmix_tm_none_kernel(tc, lg, vs, v4_words, v4_scales, v8_words, v8_
         ctx.enter_context(tc.manual_schedule())
 
         units = [(h, j) for h in range(2) for j in range(j_tiles)]
-        vs_sb = keep.tile([P, 2, PACK], F32, name="vs_sb")
+        vs_sb = keep.tile([P, 2, 2 * PACK], F32, name="vs_sb")
         logits = {}
         exps = {}
         grouped = {u: keep.tile([P, J_TILE * PACK], BF16, name="grouped%d_%d" % u, align_bytes=64) for u in units}
@@ -67,6 +67,9 @@ def tile_mix_kvmix_tm_none_kernel(tc, lg, vs, v4_words, v4_scales, v8_words, v8_
             dst = paired[:, a0:a1, (j0 - paired_j) * J_TILE : (j1 - paired_j) * J_TILE, :]
             nc.scalar.activation(out=dst, in_=src.rearrange("p (a b) c -> p a c b", b=2), func=EXP)
 
+        def zero_plane(engine, h):
+            engine.memset(v_scales[h][:].bitcast(I32), 0)
+
         def load_scales(engine, h, q0=0, q1=4):
             scales = (v4_scales, v8_scales)[h]
             for q in range(q0, q1):
@@ -84,12 +87,12 @@ def tile_mix_kvmix_tm_none_kernel(tc, lg, vs, v4_words, v4_scales, v8_words, v8_
                 v_codes[(h, n)] = chunk[:, (n - n0) * per : (n - n0 + 1) * per].bitcast((FP4X4, FP8X4)[h])
 
         def load_vs(engine):
-            engine.dma_start(out=vs_sb[:], in_=vs.rearrange("(h p i) -> p h i", h=2, i=PACK))
+            engine.dma_start(out=vs_sb[:, :, :PACK], in_=vs.rearrange("(h p i) -> p h i", h=2, i=PACK))
 
         def scale(h, j, engine=nc.vector, c0=0, c1=J_TILE):
             paired, paired_j = exps[(h, j)]
             base = (j - paired_j) * J_TILE
-            factor = vs_sb[:, h, :].rearrange("p (a b) -> p a b", b=2).unsqueeze(1).to_broadcast([P, c1 - c0, 2, 2])
+            factor = vs_sb[:, h, :PACK].rearrange("p (a b) -> p a b", b=2).unsqueeze(1).to_broadcast([P, c1 - c0, 2, 2])
             engine.tensor_tensor(
                 out=grouped[(h, j)][:, PACK * c0 : PACK * c1].rearrange("p (c a b) -> p c a b", a=2, b=2),
                 in0=paired[:, :, base + c0 : base + c1, :].rearrange("p a c b -> p c a b"),
@@ -131,32 +134,27 @@ def tile_mix_kvmix_tm_none_kernel(tc, lg, vs, v4_words, v4_scales, v8_words, v8_
             copy_out(j, n, engine)
             store(j, n * N_TILE, (n + 1) * N_TILE)
 
-        nc.vector.memset(v_scales[0][:].bitcast(I32), 0)
-        nc.gpsimd.memset(v_scales[1][:].bitcast(I32), 0)
+        zero_plane(nc.vector, 0)
+        zero_plane(nc.gpsimd, 1)
         load_scales(nc.gpsimd, 1, 0, 4)
-        load_lg(0, 0, 2, 0, 1)
-        load_lg(0, 0, 2, 1, 2)
+        load_lg(0, 0, 2, 0, 2)
         load_vs(nc.sync)
-        load_lg(1, 0, 2, 0, 1)
-        load_lg(1, 0, 2, 1, 2)
-        load_scales(nc.sync, 0, 0, 2)
-        load_lg(0, 2, 4, 0, 1)
-        load_scales(nc.sync, 0, 2, 4)
+        load_lg(1, 0, 2, 0, 2)
+        load_scales(nc.sync, 0, 0, 4)
         load_v(0, 0, 2)
+        load_lg(0, 2, 4, 0, 1)
         load_lg(0, 2, 4, 1, 2)
         load_v(1, 0, 1)
         load_lg(1, 2, 4, 0, 1)
         load_lg(1, 2, 4, 1, 2)
         load_v(1, 1, 2)
-        exponentiate(0, 0, 2, 0, 1)
-        exponentiate(0, 0, 1, 1, 2)
-        exponentiate(0, 1, 2, 1, 2)
+        exponentiate(0, 0, 1, 0, 2)
+        exponentiate(0, 1, 2, 0, 2)
         scale(0, 0)
-        exponentiate(1, 0, 2, 0, 1)
+        exponentiate(1, 0, 1, 0, 2)
         scale(0, 1)
         quantize(0, 0)
-        exponentiate(1, 0, 1, 1, 2)
-        exponentiate(1, 1, 2, 1, 2)
+        exponentiate(1, 1, 2, 0, 2)
         scale(1, 0)
         quantize(0, 1)
         exponentiate(0, 2, 4, 0, 1)

@@ -40,8 +40,8 @@ def tile_mix_kvmix_tm_none_kernel(tc, lg, vs, v4_words, v4_scales, v8_words, v8_
         e_codes = {u: keep.tile([P, J_TILE], U32, name="e_codes%d_%d" % u, align_bytes=64) for u in units}
         e_scales = {u: keep.tile([P, J_TILE], U8, name="e_scales%d_%d" % u, align_bytes=64) for u in units}
         v_codes = {}
-        v_scales = [keep.tile([P, D], U8, name="v_scales%d" % h, align_bytes=64) for h in range(2)]
-        results = [keep.tile([P, D], F32, name="results%d" % j) for j in range(j_tiles)]
+        v_scales = [keep.tile([P, D], U8, name="v_scales%d" % h, align_bytes=256) for h in range(2)]
+        results = [keep.tile([P, D], F32, name="results%d" % j, align_bytes=256) for j in range(j_tiles)]
         accs = [
             [psum.tile([P, N_TILE], F32, name="acc%d_%d" % (j, n)) for n in range(n_tiles)] for j in range(j_tiles)
         ]
@@ -49,7 +49,7 @@ def tile_mix_kvmix_tm_none_kernel(tc, lg, vs, v4_words, v4_scales, v8_words, v8_
 
         def load_lg(h, j0, j1, a0=0, a1=2, engine=nc.sync):
             width = (j1 - j0) * J_TILE
-            chunk = keep.tile([P, 2 * (a1 - a0), width], F32, name="lg%d_%d_%d" % (h, j0, a0))
+            chunk = keep.tile([P, 2 * (a1 - a0), width], F32, name="lg%d_%d_%d" % (h, j0, a0), align_bytes=256)
             rows = lg[h * HALF : (h + 1) * HALF, j0 * J_TILE : j1 * J_TILE].rearrange("(p i) j -> p i j", i=PACK)
             engine.dma_start(out=chunk[:], in_=rows[:, 2 * a0 : 2 * a1, :])
             if (h, j0) not in exps:
@@ -81,7 +81,7 @@ def tile_mix_kvmix_tm_none_kernel(tc, lg, vs, v4_words, v4_scales, v8_words, v8_
         def load_v(h, n0, n1, engine=nc.sync):
             per = (2, 4)[h] * N_TILE
             words = v4_words[0] if h == 0 else v8_words[0].rearrange("p n t -> p (n t)")
-            chunk = keep.tile([P, (n1 - n0) * per], U8, name="v%d_%d" % (h, n0), align_bytes=64)
+            chunk = keep.tile([P, (n1 - n0) * per], U8, name="v%d_%d" % (h, n0), align_bytes=256)
             engine.dma_start(out=chunk[:].bitcast(I32), in_=words[:, n0 * per : n1 * per].bitcast(I32))
             for n in range(n0, n1):
                 v_codes[(h, n)] = chunk[:, (n - n0) * per : (n - n0 + 1) * per].bitcast((FP4X4, FP8X4)[h])

@@ -141,12 +141,12 @@ def tile_mix_kvmix_tm_none_kernel(tc, lg, vs, v4_words, v4_scales, v8_words, v8_
         load_vs(nc.sync)
         load_lg(1, 0, 2, 0, 2)
         load_scales(nc.sync, 0, 0, 4)
+        load_lg(0, 2, 3, 0, 2)
         load_v(0, 0, 2)
-        load_lg(0, 2, 4, 0, 1)
-        load_lg(0, 2, 4, 1, 2)
+        load_lg(1, 2, 3, 0, 2)
         load_v(1, 0, 1)
-        load_lg(1, 2, 4, 0, 1)
-        load_lg(1, 2, 4, 1, 2)
+        load_lg(0, 3, 4, 0, 2)
+        load_lg(1, 3, 4, 0, 2)
         load_v(1, 1, 2)
         exponentiate(0, 0, 1, 0, 2)
         exponentiate(0, 1, 2, 0, 2)
@@ -157,44 +157,42 @@ def tile_mix_kvmix_tm_none_kernel(tc, lg, vs, v4_words, v4_scales, v8_words, v8_
         exponentiate(1, 1, 2, 0, 2)
         scale(1, 0)
         quantize(0, 1)
-        exponentiate(0, 2, 4, 0, 1)
+        exponentiate(0, 2, 3, 0, 2)
         scale(1, 1)
         quantize(1, 0)
-        exponentiate(0, 2, 3, 1, 2)
-        exponentiate(0, 3, 4, 1, 2)
+        exponentiate(1, 2, 3, 0, 2)
+        scale(0, 2)
         quantize(1, 1)
         multiply(0, 0, 0)
-        multiply(0, 0, 1)
         multiply(0, 1, 0)
-        scale(0, 2)
+        multiply(0, 0, 1)
+        scale(1, 2)
+        quantize(0, 2)
+        quantize(1, 2)
         multiply(1, 0, 0)
         multiply(1, 1, 0)
-        exponentiate(1, 2, 4, 0, 1)
-        scale(0, 3)
-        quantize(0, 2)
-        multiply(0, 1, 1)
-        drain(0, 0, "vector")
-        exponentiate(1, 2, 3, 1, 2)
-        exponentiate(1, 3, 4, 1, 2)
         multiply(0, 2, 0)
-        drain(1, 0, "scalar")
-        scale(1, 2)
-        multiply(1, 0, 1)
-        multiply(1, 1, 1)
-        quantize(0, 3)
-        multiply(0, 2, 1)
-        drain(0, 1, "scalar")
-        quantize(1, 2)
         multiply(1, 2, 0)
+        exponentiate(0, 3, 4, 0, 2)
+        drain(0, 0, "vector")
+        exponentiate(1, 3, 4, 0, 2)
+        drain(1, 0, "scalar")
+        scale(0, 3)
+        drain(2, 0, "scalar")
+        multiply(1, 0, 1)
+        multiply(0, 1, 1)
+        multiply(1, 1, 1)
+        multiply(0, 2, 1)
         multiply(1, 2, 1)
         scale(1, 3)
-        multiply(0, 3, 0)
-        multiply(0, 3, 1)
-        drain(1, 1, "scalar")
+        quantize(0, 3)
         quantize(1, 3)
+        multiply(0, 3, 0)
         multiply(1, 3, 0)
+        multiply(0, 3, 1)
         multiply(1, 3, 1)
-        drain(2, 0, "scalar")
+        drain(0, 1, "scalar")
+        drain(1, 1, "scalar")
         drain(2, 1, "vector")
         drain(3, 0, "vector")
         drain(3, 1, "scalar")

@@ -165,21 +165,22 @@ def tile_mix_kvmix_tm_none_kernel(tc, lg, vs, v4_words, v4_scales, v8_words, v8_
         quantize(1, 1)
         multiply(0, 0, 0)
         multiply(0, 1, 0)
-        multiply(0, 0, 1)
         scale(1, 2)
         quantize(0, 2)
-        quantize(1, 2)
         multiply(1, 0, 0)
         multiply(1, 1, 0)
-        multiply(0, 2, 0)
-        multiply(1, 2, 0)
         exponentiate(0, 3, 4, 0, 2)
         drain(0, 0, "vector")
+        quantize(1, 2)
+        multiply(0, 0, 1)
+        multiply(1, 0, 1)
+        multiply(0, 2, 0)
+        multiply(1, 2, 0)
         exponentiate(1, 3, 4, 0, 2)
         drain(1, 0, "scalar")
         scale(0, 3)
+        drain(0, 1, "scalar")
         drain(2, 0, "scalar")
-        multiply(1, 0, 1)
         multiply(0, 1, 1)
         multiply(1, 1, 1)
         multiply(0, 2, 1)
@@ -191,8 +192,7 @@ def tile_mix_kvmix_tm_none_kernel(tc, lg, vs, v4_words, v4_scales, v8_words, v8_
         multiply(1, 3, 0)
         multiply(0, 3, 1)
         multiply(1, 3, 1)
-        drain(0, 1, "scalar")
         drain(1, 1, "scalar")
         drain(2, 1, "vector")
-        drain(3, 0, "vector")
-        drain(3, 1, "scalar")
+        drain(3, 0, "scalar")
+        drain(3, 1, "vector")

@@ -141,58 +141,58 @@ def tile_mix_kvmix_tm_none_kernel(tc, lg, vs, v4_words, v4_scales, v8_words, v8_
         load_vs(nc.sync)
         load_lg(1, 0, 2, 0, 2)
         load_scales(nc.sync, 0, 0, 4)
-        load_lg(0, 2, 3, 0, 2)
         load_v(0, 0, 2)
+        load_lg(0, 2, 3, 0, 2)
         load_lg(1, 2, 3, 0, 2)
         load_v(1, 0, 1)
         load_lg(0, 3, 4, 0, 2)
-        load_lg(1, 3, 4, 0, 2)
         load_v(1, 1, 2)
+        load_lg(1, 3, 4, 0, 2)
         exponentiate(0, 0, 1, 0, 2)
         exponentiate(0, 1, 2, 0, 2)
         scale(0, 0)
-        exponentiate(1, 0, 1, 0, 2)
         scale(0, 1)
+        exponentiate(1, 0, 1, 0, 2)
         quantize(0, 0)
         exponentiate(1, 1, 2, 0, 2)
         scale(1, 0)
         quantize(0, 1)
-        exponentiate(0, 2, 3, 0, 2)
         scale(1, 1)
         quantize(1, 0)
-        exponentiate(1, 2, 3, 0, 2)
-        scale(0, 2)
         quantize(1, 1)
         multiply(0, 0, 0)
         multiply(0, 1, 0)
+        exponentiate(0, 2, 3, 0, 2)
+        exponentiate(1, 2, 3, 0, 2)
+        scale(0, 2)
         scale(1, 2)
-        quantize(0, 2)
         multiply(1, 0, 0)
         multiply(1, 1, 0)
-        exponentiate(0, 3, 4, 0, 2)
+        multiply(0, 0, 1)
+        quantize(0, 2)
         drain(0, 0, "vector")
         quantize(1, 2)
-        multiply(0, 0, 1)
+        exponentiate(0, 3, 4, 0, 2)
+        drain(1, 0, "scalar")
         multiply(1, 0, 1)
         multiply(0, 2, 0)
         multiply(1, 2, 0)
-        exponentiate(1, 3, 4, 0, 2)
-        drain(1, 0, "scalar")
-        scale(0, 3)
-        drain(0, 1, "scalar")
-        drain(2, 0, "scalar")
-        multiply(0, 1, 1)
-        multiply(1, 1, 1)
         multiply(0, 2, 1)
         multiply(1, 2, 1)
+        multiply(0, 1, 1)
+        multiply(1, 1, 1)
+        scale(0, 3)
+        drain(0, 1, "vector")
+        exponentiate(1, 3, 4, 0, 2)
         scale(1, 3)
         quantize(0, 3)
         quantize(1, 3)
+        drain(2, 0, "scalar")
+        drain(2, 1, "scalar")
+        drain(1, 1, "vector")
         multiply(0, 3, 0)
         multiply(1, 3, 0)
         multiply(0, 3, 1)
         multiply(1, 3, 1)
-        drain(1, 1, "scalar")
-        drain(2, 1, "vector")
         drain(3, 0, "scalar")
         drain(3, 1, "vector")

@@ -25,7 +25,6 @@ MULT = mybir.AluOpType.mult
 def tile_mix_kvmix_tm_none_kernel(tc, lg, vs, v4_words, v4_scales, v8_words, v8_scales, out):
     nc = tc.nc
     j_tiles = J // J_TILE
-    n_tiles = D // N_TILE
 
     with ExitStack() as ctx:
         keep = ctx.enter_context(tc.tile_pool(name="keep", bufs=1))
@@ -42,10 +41,7 @@ def tile_mix_kvmix_tm_none_kernel(tc, lg, vs, v4_words, v4_scales, v8_words, v8_
         v_codes = {}
         v_scales = [keep.tile([P, D], U8, name="v_scales%d" % h, align_bytes=256) for h in range(2)]
         results = [keep.tile([P, D], F32, name="results%d" % j, align_bytes=256) for j in range(j_tiles)]
-        accs = [
-            [psum.tile([P, N_TILE], F32, name="acc%d_%d" % (j, n)) for n in range(n_tiles)] for j in range(j_tiles)
-        ]
-        opened = set()
+        accs = {}
 
         def load_lg(h, j0, j1, a0=0, a1=2, engine=nc.sync):
             width = (j1 - j0) * J_TILE
@@ -60,11 +56,11 @@ def tile_mix_kvmix_tm_none_kernel(tc, lg, vs, v4_words, v4_scales, v8_words, v8_
                 for a in range(a0, a1):
                     logits[(h, j, a)] = (chunk, j0, a0)
 
-        def exponentiate(h, j0, j1, a0=0, a1=2):
-            chunk, first_j, first_a = logits[(h, j0, a0)]
-            paired, paired_j = exps[(h, j0)]
-            src = chunk[:, 2 * (a0 - first_a) : 2 * (a1 - first_a), (j0 - first_j) * J_TILE : (j1 - first_j) * J_TILE]
-            dst = paired[:, a0:a1, (j0 - paired_j) * J_TILE : (j1 - paired_j) * J_TILE, :]
+        def exponentiate(h, j, c0=0, c1=J_TILE, a0=0, a1=2):
+            chunk, first_j, first_a = logits[(h, j, a0)]
+            paired, paired_j = exps[(h, j)]
+            src = chunk[:, 2 * (a0 - first_a) : 2 * (a1 - first_a), (j - first_j) * J_TILE + c0 : (j - first_j) * J_TILE + c1]
+            dst = paired[:, a0:a1, (j - paired_j) * J_TILE + c0 : (j - paired_j) * J_TILE + c1, :]
             nc.scalar.activation(out=dst, in_=src.rearrange("p (a b) c -> p a c b", b=2), func=EXP)
 
         def zero_plane(engine, h):
@@ -84,7 +80,7 @@ def tile_mix_kvmix_tm_none_kernel(tc, lg, vs, v4_words, v4_scales, v8_words, v8_
             chunk = keep.tile([P, (n1 - n0) * per], U8, name="v%d_%d" % (h, n0), align_bytes=256)
             engine.dma_start(out=chunk[:].bitcast(I32), in_=words[:, n0 * per : n1 * per].bitcast(I32))
             for n in range(n0, n1):
-                v_codes[(h, n)] = chunk[:, (n - n0) * per : (n - n0 + 1) * per].bitcast((FP4X4, FP8X4)[h])
+                v_codes[(h, n)] = (chunk, n0 * N_TILE)
 
         def load_vs(engine):
             engine.dma_start(out=vs_sb[:, :, :PACK], in_=vs.rearrange("(h p i) -> p h i", h=2, i=PACK))
@@ -100,39 +96,42 @@ def tile_mix_kvmix_tm_none_kernel(tc, lg, vs, v4_words, v4_scales, v8_words, v8_
                 op=MULT,
             )
 
-        def quantize(h, j):
+        def quantize(h, j, c0=0, c1=J_TILE):
             nc.vector.quantize_mx(
-                out=e_codes[(h, j)][:].bitcast(FP8X4),
-                scales=e_scales[(h, j)][:],
-                in_=grouped[(h, j)][:],
+                out=e_codes[(h, j)][:, c0:c1].bitcast(FP8X4),
+                scales=e_scales[(h, j)][:, c0:c1],
+                in_=grouped[(h, j)][:, PACK * c0 : PACK * c1],
             )
 
-        def multiply(h, j, n):
-            first = (j, n) not in opened
-            opened.add((j, n))
+        def multiply(h, j, d0, d1, bank=None):
+            first = (j, d0) not in accs
+            if first:
+                accs[(j, d0)] = psum.tile([P, d1 - d0], F32, name="acc%d_%d" % (j, d0), tag=bank)
+            words, first_d = v_codes[(h, d0 // N_TILE)]
+            per = (2, 4)[h]
             nc.tensor.matmul_mx(
-                out=accs[j][n][:],
+                out=accs[(j, d0)][:],
                 lhsT=e_codes[(h, j)][:].bitcast(FP8X4),
                 lhsT_scale=e_scales[(h, j)][:],
-                rhs=v_codes[(h, n)],
-                rhs_scale=v_scales[h][4 * h :, n * N_TILE : (n + 1) * N_TILE],
+                rhs=words[:, per * (d0 - first_d) : per * (d1 - first_d)].bitcast((FP4X4, FP8X4)[h]),
+                rhs_scale=v_scales[h][4 * h :, d0:d1],
                 start=first,
                 stop=not first,
             )
 
-        def copy_out(j, n, engine, c0=0, c1=N_TILE):
-            dst = results[j][:, n * N_TILE + c0 : n * N_TILE + c1]
+        def copy_out(j, d0, d1, engine):
+            dst = results[j][:, d0:d1]
             if engine == "scalar":
-                nc.scalar.copy(out=dst, in_=accs[j][n][:, c0:c1])
+                nc.scalar.copy(out=dst, in_=accs[(j, d0)][:])
             else:
-                nc.vector.tensor_copy(out=dst, in_=accs[j][n][:, c0:c1])
+                nc.vector.tensor_copy(out=dst, in_=accs[(j, d0)][:])
 
         def store(j, c0, c1, engine=nc.sync):
             engine.dma_start(out=out[j * J_TILE : (j + 1) * J_TILE, c0:c1], in_=results[j][:, c0:c1])
 
-        def drain(j, n, engine):
-            copy_out(j, n, engine)
-            store(j, n * N_TILE, (n + 1) * N_TILE)
+        def drain(j, d0, d1, engine):
+            copy_out(j, d0, d1, engine)
+            store(j, d0, d1)
 
         zero_plane(nc.vector, 0)
         zero_plane(nc.gpsimd, 1)
@@ -140,59 +139,71 @@ def tile_mix_kvmix_tm_none_kernel(tc, lg, vs, v4_words, v4_scales, v8_words, v8_
         load_lg(0, 0, 2, 0, 2)
         load_vs(nc.sync)
         load_lg(1, 0, 2, 0, 2)
-        load_scales(nc.sync, 0, 0, 4)
-        load_v(0, 0, 2)
         load_lg(0, 2, 3, 0, 2)
+        load_scales(nc.sync, 0, 0, 4)
+        load_v(0, 0, 1)
         load_lg(1, 2, 3, 0, 2)
         load_v(1, 0, 1)
         load_lg(0, 3, 4, 0, 2)
+        load_v(0, 1, 2)
         load_v(1, 1, 2)
         load_lg(1, 3, 4, 0, 2)
-        exponentiate(0, 0, 1, 0, 2)
-        exponentiate(0, 1, 2, 0, 2)
+        exponentiate(0, 0)
+        exponentiate(0, 1)
         scale(0, 0)
         scale(0, 1)
-        exponentiate(1, 0, 1, 0, 2)
+        exponentiate(1, 0)
         quantize(0, 0)
-        exponentiate(1, 1, 2, 0, 2)
+        exponentiate(1, 1)
         scale(1, 0)
         quantize(0, 1)
+        exponentiate(0, 2)
         scale(1, 1)
         quantize(1, 0)
-        quantize(1, 1)
-        multiply(0, 0, 0)
-        multiply(0, 1, 0)
-        exponentiate(0, 2, 3, 0, 2)
-        exponentiate(1, 2, 3, 0, 2)
+        multiply(0, 0, 0, 512, "bank0")
+        multiply(0, 1, 0, 512, "bank2")
+        exponentiate(1, 2)
         scale(0, 2)
+        quantize(1, 1)
+        multiply(1, 0, 0, 512)
         scale(1, 2)
-        multiply(1, 0, 0)
-        multiply(1, 1, 0)
-        multiply(0, 0, 1)
         quantize(0, 2)
-        drain(0, 0, "vector")
-        quantize(1, 2)
-        exponentiate(0, 3, 4, 0, 2)
-        drain(1, 0, "scalar")
-        multiply(1, 0, 1)
-        multiply(0, 2, 0)
-        multiply(1, 2, 0)
-        multiply(0, 2, 1)
-        multiply(1, 2, 1)
-        multiply(0, 1, 1)
-        multiply(1, 1, 1)
+        exponentiate(0, 3)
+        multiply(1, 1, 0, 512)
+        multiply(0, 0, 512, 1024, "bank1")
+        multiply(1, 0, 512, 1024)
+        drain(0, 0, 512, "scalar")
         scale(0, 3)
-        drain(0, 1, "vector")
-        exponentiate(1, 3, 4, 0, 2)
-        scale(1, 3)
+        quantize(1, 2)
+        drain(1, 0, 512, "scalar")
+        multiply(0, 1, 512, 1024, "bank3")
+        multiply(1, 1, 512, 1024)
+        multiply(0, 2, 0, 512, "bank4")
+        multiply(1, 2, 0, 512)
+        multiply(0, 2, 512, 1024, "bank5")
+        multiply(1, 2, 512, 1024)
+        drain(0, 512, 1024, "vector")
         quantize(0, 3)
-        quantize(1, 3)
-        drain(2, 0, "scalar")
-        drain(2, 1, "scalar")
-        drain(1, 1, "vector")
-        multiply(0, 3, 0)
-        multiply(1, 3, 0)
-        multiply(0, 3, 1)
-        multiply(1, 3, 1)
-        drain(3, 0, "scalar")
-        drain(3, 1, "vector")
+        exponentiate(1, 3, 0, 64)
+        exponentiate(1, 3, 64, 128)
+        scale(1, 3, nc.vector, 0, 64)
+        scale(1, 3, nc.vector, 64, 128)
+        quantize(1, 3, 0, 64)
+        quantize(1, 3, 64, 128)
+        drain(1, 512, 1024, "scalar")
+        drain(2, 0, 512, "scalar")
+        drain(2, 512, 1024, "vector")
+        multiply(0, 3, 0, 256, "bank6")
+        multiply(0, 3, 256, 512, "bank0")
+        multiply(0, 3, 512, 768, "bank7")
+        multiply(0, 3, 768, 1024, "bank2")
+        multiply(1, 3, 0, 256)
+        multiply(1, 3, 256, 512)
+        multiply(1, 3, 512, 768)
+        multiply(1, 3, 768, 1024)
+        copy_out(3, 0, 256, "vector")
+        copy_out(3, 256, 512, "scalar")
+        store(3, 0, 512)
+        copy_out(3, 512, 768, "vector")
+        copy_out(3, 768, 1024, "scalar")
+        store(3, 512, 1024)

@@ -139,9 +139,9 @@ def tile_mix_kvmix_tm_none_kernel(tc, lg, vs, v4_words, v4_scales, v8_words, v8_
         load_lg(0, 0, 2, 0, 2)
         load_vs(nc.sync)
         load_lg(1, 0, 2, 0, 2)
-        load_lg(0, 2, 3, 0, 2)
         load_scales(nc.sync, 0, 0, 4)
         load_v(0, 0, 1)
+        load_lg(0, 2, 3, 0, 2)
         load_lg(1, 2, 3, 0, 2)
         load_v(1, 0, 1)
         load_lg(0, 3, 4, 0, 2)
@@ -154,9 +154,9 @@ def tile_mix_kvmix_tm_none_kernel(tc, lg, vs, v4_words, v4_scales, v8_words, v8_
         scale(0, 1)
         exponentiate(1, 0)
         quantize(0, 0)
+        quantize(0, 1)
         exponentiate(1, 1)
         scale(1, 0)
-        quantize(0, 1)
         exponentiate(0, 2)
         scale(1, 1)
         quantize(1, 0)
@@ -166,8 +166,8 @@ def tile_mix_kvmix_tm_none_kernel(tc, lg, vs, v4_words, v4_scales, v8_words, v8_
         scale(0, 2)
         quantize(1, 1)
         multiply(1, 0, 0, 512)
-        scale(1, 2)
         quantize(0, 2)
+        scale(1, 2)
         exponentiate(0, 3)
         multiply(1, 1, 0, 512)
         multiply(0, 0, 512, 1024, "bank1")

@@ -152,53 +152,57 @@ def tile_mix_kvmix_tm_none_kernel(tc, lg, vs, v4_words, v4_scales, v8_words, v8_
         exponentiate(0, 1)
         scale(0, 0)
         scale(0, 1)
-        exponentiate(1, 0)
         quantize(0, 0)
         quantize(0, 1)
-        exponentiate(1, 1)
+        exponentiate(1, 0)
         scale(1, 0)
-        exponentiate(0, 2)
+        exponentiate(1, 1)
         scale(1, 1)
         quantize(1, 0)
-        multiply(0, 0, 0, 512, "bank0")
-        multiply(0, 1, 0, 512, "bank2")
-        exponentiate(1, 2)
-        scale(0, 2)
         quantize(1, 1)
-        multiply(1, 0, 0, 512)
-        quantize(0, 2)
+        multiply(0, 0, 0, 256, "bank0")
+        multiply(0, 0, 256, 512, "bank7")
+        multiply(0, 1, 0, 512, "bank2")
+        exponentiate(0, 2)
+        scale(0, 2)
+        exponentiate(1, 2)
         scale(1, 2)
-        exponentiate(0, 3)
+        multiply(1, 0, 0, 256)
+        multiply(1, 0, 256, 512)
         multiply(1, 1, 0, 512)
+        exponentiate(0, 3)
+        copy_out(0, 0, 256, "vector")
+        copy_out(0, 256, 512, "scalar")
+        store(0, 0, 512)
+        drain(1, 0, 512, "scalar")
         multiply(0, 0, 512, 1024, "bank1")
         multiply(1, 0, 512, 1024)
-        drain(0, 0, 512, "scalar")
-        scale(0, 3)
-        quantize(1, 2)
-        drain(1, 0, 512, "scalar")
         multiply(0, 1, 512, 1024, "bank3")
         multiply(1, 1, 512, 1024)
+        quantize(0, 2)
+        quantize(1, 2)
+        scale(0, 3)
         multiply(0, 2, 0, 512, "bank4")
         multiply(1, 2, 0, 512)
         multiply(0, 2, 512, 1024, "bank5")
         multiply(1, 2, 512, 1024)
         drain(0, 512, 1024, "vector")
-        quantize(0, 3)
         exponentiate(1, 3, 0, 64)
         exponentiate(1, 3, 64, 128)
         scale(1, 3, nc.vector, 0, 64)
         scale(1, 3, nc.vector, 64, 128)
+        quantize(0, 3)
         quantize(1, 3, 0, 64)
         quantize(1, 3, 64, 128)
         drain(1, 512, 1024, "scalar")
         drain(2, 0, 512, "scalar")
-        drain(2, 512, 1024, "vector")
+        drain(2, 512, 1024, "scalar")
         multiply(0, 3, 0, 256, "bank6")
         multiply(0, 3, 256, 512, "bank0")
-        multiply(0, 3, 512, 768, "bank7")
-        multiply(0, 3, 768, 1024, "bank2")
         multiply(1, 3, 0, 256)
         multiply(1, 3, 256, 512)
+        multiply(0, 3, 512, 768, "bank7")
+        multiply(0, 3, 768, 1024, "bank2")
         multiply(1, 3, 512, 768)
         multiply(1, 3, 768, 1024)
         copy_out(3, 0, 256, "vector")

@@ -33,8 +33,8 @@ def tile_mix_kvmix_tm_none_kernel(tc, lg, vs, v4_words, v4_scales, v8_words, v8_
 
         units = [(h, j) for h in range(2) for j in range(j_tiles)]
         vs_sb = keep.tile([P, 2, 2 * PACK], F32, name="vs_sb")
-        logits = {}
-        exps = {}
+        logits = [[], []]
+        exps = {u: keep.tile([P, 2, J_TILE, 2], F32, name="exps%d_%d" % u) for u in units}
         grouped = {u: keep.tile([P, J_TILE * PACK], BF16, name="grouped%d_%d" % u, align_bytes=64) for u in units}
         e_codes = {u: keep.tile([P, J_TILE], U32, name="e_codes%d_%d" % u, align_bytes=64) for u in units}
         e_scales = {u: keep.tile([P, J_TILE], U8, name="e_scales%d_%d" % u, align_bytes=64) for u in units}
@@ -43,25 +43,16 @@ def tile_mix_kvmix_tm_none_kernel(tc, lg, vs, v4_words, v4_scales, v8_words, v8_
         results = [keep.tile([P, D], F32, name="results%d" % j, align_bytes=256) for j in range(j_tiles)]
         accs = {}
 
-        def load_lg(h, j0, j1, a0=0, a1=2, engine=nc.sync):
-            width = (j1 - j0) * J_TILE
-            chunk = keep.tile([P, 2 * (a1 - a0), width], F32, name="lg%d_%d_%d" % (h, j0, a0), align_bytes=256)
-            rows = lg[h * HALF : (h + 1) * HALF, j0 * J_TILE : j1 * J_TILE].rearrange("(p i) j -> p i j", i=PACK)
-            engine.dma_start(out=chunk[:], in_=rows[:, 2 * a0 : 2 * a1, :])
-            if (h, j0) not in exps:
-                paired = keep.tile([P, 2, width, 2], F32, name="exps%d_%d" % (h, j0))
-                for j in range(j0, j1):
-                    exps[(h, j)] = (paired, j0)
-            for j in range(j0, j1):
-                for a in range(a0, a1):
-                    logits[(h, j, a)] = (chunk, j0, a0)
+        def load_lg(h, c0, c1):
+            chunk = keep.tile([P, PACK, c1 - c0], F32, name="lg%d_%d" % (h, c0), align_bytes=256)
+            rows = lg[h * HALF : (h + 1) * HALF, c0:c1].rearrange("(p i) j -> p i j", i=PACK)
+            nc.sync.dma_start(out=chunk[:], in_=rows)
+            logits[h].append((c0, c1, chunk))
 
-        def exponentiate(h, j, c0=0, c1=J_TILE, a0=0, a1=2):
-            chunk, first_j, first_a = logits[(h, j, a0)]
-            paired, paired_j = exps[(h, j)]
-            src = chunk[:, 2 * (a0 - first_a) : 2 * (a1 - first_a), (j - first_j) * J_TILE + c0 : (j - first_j) * J_TILE + c1]
-            dst = paired[:, a0:a1, (j - paired_j) * J_TILE + c0 : (j - paired_j) * J_TILE + c1, :]
-            nc.scalar.activation(out=dst, in_=src.rearrange("p (a b) c -> p a c b", b=2), func=EXP)
+        def exponentiate(h, j, c0=0, c1=J_TILE):
+            first, chunk = [(a, t) for a, b, t in logits[h] if a <= j * J_TILE + c0 < b][0]
+            src = chunk[:, :, j * J_TILE + c0 - first : j * J_TILE + c1 - first]
+            nc.scalar.activation(out=exps[(h, j)][:, :, c0:c1, :], in_=src.rearrange("p (a b) c -> p a c b", b=2), func=EXP)
 
         def zero_plane(engine, h):
             engine.memset(v_scales[h][:].bitcast(I32), 0)
@@ -86,12 +77,10 @@ def tile_mix_kvmix_tm_none_kernel(tc, lg, vs, v4_words, v4_scales, v8_words, v8_
             engine.dma_start(out=vs_sb[:, :, :PACK], in_=vs.rearrange("(h p i) -> p h i", h=2, i=PACK))
 
         def scale(h, j, engine=nc.vector, c0=0, c1=J_TILE):
-            paired, paired_j = exps[(h, j)]
-            base = (j - paired_j) * J_TILE
             factor = vs_sb[:, h, :PACK].rearrange("p (a b) -> p a b", b=2).unsqueeze(1).to_broadcast([P, c1 - c0, 2, 2])
             engine.tensor_tensor(
                 out=grouped[(h, j)][:, PACK * c0 : PACK * c1].rearrange("p (c a b) -> p c a b", a=2, b=2),
-                in0=paired[:, :, base + c0 : base + c1, :].rearrange("p a c b -> p c a b"),
+                in0=exps[(h, j)][:, :, c0:c1, :].rearrange("p a c b -> p c a b"),
                 in1=factor,
                 op=MULT,
             )
@@ -136,18 +125,18 @@ def tile_mix_kvmix_tm_none_kernel(tc, lg, vs, v4_words, v4_scales, v8_words, v8_
         zero_plane(nc.vector, 0)
         zero_plane(nc.gpsimd, 1)
         load_scales(nc.gpsimd, 1, 0, 4)
-        load_lg(0, 0, 2, 0, 2)
+        load_lg(0, 0, 256)
         load_vs(nc.sync)
-        load_lg(1, 0, 2, 0, 2)
+        load_lg(1, 0, 256)
         load_scales(nc.sync, 0, 0, 4)
         load_v(0, 0, 1)
-        load_lg(0, 2, 3, 0, 2)
-        load_lg(1, 2, 3, 0, 2)
+        load_lg(0, 256, 384)
+        load_lg(1, 256, 384)
         load_v(1, 0, 1)
-        load_lg(0, 3, 4, 0, 2)
+        load_lg(0, 384, 512)
         load_v(0, 1, 2)
         load_v(1, 1, 2)
-        load_lg(1, 3, 4, 0, 2)
+        load_lg(1, 384, 512)
         exponentiate(0, 0)
         exponentiate(0, 1)
         scale(0, 0)
@@ -161,48 +150,52 @@ def tile_mix_kvmix_tm_none_kernel(tc, lg, vs, v4_words, v4_scales, v8_words, v8_
         quantize(1, 0)
         quantize(1, 1)
         multiply(0, 0, 0, 256, "bank0")
-        multiply(0, 0, 256, 512, "bank7")
+        multiply(0, 0, 256, 512, "bank1")
         multiply(0, 1, 0, 512, "bank2")
+        multiply(1, 0, 0, 256)
+        multiply(1, 0, 256, 512)
+        multiply(1, 1, 0, 512)
         exponentiate(0, 2)
         scale(0, 2)
         exponentiate(1, 2)
         scale(1, 2)
-        multiply(1, 0, 0, 256)
-        multiply(1, 0, 256, 512)
-        multiply(1, 1, 0, 512)
         exponentiate(0, 3)
         copy_out(0, 0, 256, "vector")
         copy_out(0, 256, 512, "scalar")
         store(0, 0, 512)
         drain(1, 0, 512, "scalar")
-        multiply(0, 0, 512, 1024, "bank1")
-        multiply(1, 0, 512, 1024)
-        multiply(0, 1, 512, 1024, "bank3")
-        multiply(1, 1, 512, 1024)
         quantize(0, 2)
         quantize(1, 2)
+        multiply(0, 0, 512, 768, "bank3")
+        multiply(0, 0, 768, 1024, "bank4")
+        multiply(0, 1, 512, 1024, "bank5")
+        multiply(1, 0, 512, 768)
+        multiply(1, 0, 768, 1024)
+        multiply(1, 1, 512, 1024)
         scale(0, 3)
-        multiply(0, 2, 0, 512, "bank4")
+        multiply(0, 2, 0, 512, "bank6")
         multiply(1, 2, 0, 512)
-        multiply(0, 2, 512, 1024, "bank5")
+        multiply(0, 2, 512, 1024, "bank7")
         multiply(1, 2, 512, 1024)
-        drain(0, 512, 1024, "vector")
+        copy_out(0, 512, 768, "vector")
+        quantize(0, 3)
         exponentiate(1, 3, 0, 64)
         exponentiate(1, 3, 64, 128)
+        copy_out(0, 768, 1024, "scalar")
+        store(0, 512, 1024)
         scale(1, 3, nc.vector, 0, 64)
         scale(1, 3, nc.vector, 64, 128)
-        quantize(0, 3)
         quantize(1, 3, 0, 64)
         quantize(1, 3, 64, 128)
         drain(1, 512, 1024, "scalar")
         drain(2, 0, 512, "scalar")
-        drain(2, 512, 1024, "scalar")
-        multiply(0, 3, 0, 256, "bank6")
-        multiply(0, 3, 256, 512, "bank0")
+        drain(2, 512, 1024, "vector")
+        multiply(0, 3, 0, 256, "bank0")
+        multiply(0, 3, 256, 512, "bank1")
+        multiply(0, 3, 512, 768, "bank2")
         multiply(1, 3, 0, 256)
         multiply(1, 3, 256, 512)
-        multiply(0, 3, 512, 768, "bank7")
-        multiply(0, 3, 768, 1024, "bank2")
+        multiply(0, 3, 768, 1024, "bank3")
         multiply(1, 3, 512, 768)
         multiply(1, 3, 768, 1024)
         copy_out(3, 0, 256, "vector")

from contextlib import ExitStack

import concourse.mybir as mybir

T, J, D = 1024, 512, 1024
P = 128
PACK = 4
HALF = P * PACK
J_TILE = 128
N_TILE = 512

FLOPS = 2 * T * J * D

F32 = mybir.dt.float32
BF16 = mybir.dt.bfloat16
I32 = mybir.dt.int32
U32 = mybir.dt.uint32
U8 = mybir.dt.uint8
FP8X4 = mybir.dt.float8_e4m3fn_x4
FP4X4 = mybir.dt.float4_e2m1fn_x4
EXP = mybir.ActivationFunctionType.Exp
MULT = mybir.AluOpType.mult


def tile_mix_kvmix_tm_none_kernel(tc, lg, vs, v4_words, v4_scales, v8_words, v8_scales, out):
    nc = tc.nc
    j_tiles = J // J_TILE

    with ExitStack() as ctx:
        keep = ctx.enter_context(tc.tile_pool(name="keep", bufs=1))
        psum = ctx.enter_context(tc.psum_pool(name="psum", bufs=1))
        ctx.enter_context(tc.manual_schedule())

        units = [(h, j) for h in range(2) for j in range(j_tiles)]
        vs_sb = keep.tile([P, 2, 2 * PACK], F32, name="vs_sb")
        logits = [[], []]
        exps = {u: keep.tile([P, 2, J_TILE, 2], F32, name="exps%d_%d" % u) for u in units}
        grouped = {u: keep.tile([P, J_TILE * PACK], BF16, name="grouped%d_%d" % u, align_bytes=64) for u in units}
        e_codes = {u: keep.tile([P, J_TILE], U32, name="e_codes%d_%d" % u, align_bytes=64) for u in units}
        e_scales = {u: keep.tile([P, J_TILE], U8, name="e_scales%d_%d" % u, align_bytes=64) for u in units}
        v_codes = {}
        v_scales = [keep.tile([P, D], U8, name="v_scales%d" % h, align_bytes=256) for h in range(2)]
        results = [keep.tile([P, D], F32, name="results%d" % j, align_bytes=256) for j in range(j_tiles)]
        accs = {}

        def load_lg(h, c0, c1):
            chunk = keep.tile([P, PACK, c1 - c0], F32, name="lg%d_%d" % (h, c0), align_bytes=256)
            rows = lg[h * HALF : (h + 1) * HALF, c0:c1].rearrange("(p i) j -> p i j", i=PACK)
            nc.sync.dma_start(out=chunk[:], in_=rows)
            logits[h].append((c0, c1, chunk))

        def exponentiate(h, j, c0=0, c1=J_TILE):
            first, chunk = [(a, t) for a, b, t in logits[h] if a <= j * J_TILE + c0 < b][0]
            src = chunk[:, :, j * J_TILE + c0 - first : j * J_TILE + c1 - first]
            nc.scalar.activation(out=exps[(h, j)][:, :, c0:c1, :], in_=src.rearrange("p (a b) c -> p a c b", b=2), func=EXP)

        def zero_plane(engine, h):
            engine.memset(v_scales[h][:].bitcast(I32), 0)

        def load_scales(engine, h, q0=0, q1=4):
            scales = (v4_scales, v8_scales)[h]
            for q in range(q0, q1):
                engine.dma_start(
                    out=v_scales[h][4 * h + q : P : 32, :].bitcast(I32),
                    in_=scales[0, q:16:4, :].bitcast(I32),
                )

        def load_v(h, n0, n1, engine=nc.sync):
            per = (2, 4)[h] * N_TILE
            words = v4_words[0] if h == 0 else v8_words[0].rearrange("p n t -> p (n t)")
            chunk = keep.tile([P, (n1 - n0) * per], U8, name="v%d_%d" % (h, n0), align_bytes=256)
            engine.dma_start(out=chunk[:].bitcast(I32), in_=words[:, n0 * per : n1 * per].bitcast(I32))
            for n in range(n0, n1):
                v_codes[(h, n)] = (chunk, n0 * N_TILE)

        def load_vs(engine):
            engine.dma_start(out=vs_sb[:, :, :PACK], in_=vs.rearrange("(h p i) -> p h i", h=2, i=PACK))

        def scale(h, j, engine=nc.vector, c0=0, c1=J_TILE):
            factor = vs_sb[:, h, :PACK].rearrange("p (a b) -> p a b", b=2).unsqueeze(1).to_broadcast([P, c1 - c0, 2, 2])
            engine.tensor_tensor(
                out=grouped[(h, j)][:, PACK * c0 : PACK * c1].rearrange("p (c a b) -> p c a b", a=2, b=2),
                in0=exps[(h, j)][:, :, c0:c1, :].rearrange("p a c b -> p c a b"),
                in1=factor,
                op=MULT,
            )

        def quantize(h, j, c0=0, c1=J_TILE):
            nc.vector.quantize_mx(
                out=e_codes[(h, j)][:, c0:c1].bitcast(FP8X4),
                scales=e_scales[(h, j)][:, c0:c1],
                in_=grouped[(h, j)][:, PACK * c0 : PACK * c1],
            )

        def multiply(h, j, d0, d1, bank=None):
            first = (j, d0) not in accs
            if first:
                accs[(j, d0)] = psum.tile([P, d1 - d0], F32, name="acc%d_%d" % (j, d0), tag=bank)
            words, first_d = v_codes[(h, d0 // N_TILE)]
            per = (2, 4)[h]
            nc.tensor.matmul_mx(
                out=accs[(j, d0)][:],
                lhsT=e_codes[(h, j)][:].bitcast(FP8X4),
                lhsT_scale=e_scales[(h, j)][:],
                rhs=words[:, per * (d0 - first_d) : per * (d1 - first_d)].bitcast((FP4X4, FP8X4)[h]),
                rhs_scale=v_scales[h][4 * h :, d0:d1],
                start=first,
                stop=not first,
            )

        def copy_out(j, d0, d1, engine):
            dst = results[j][:, d0:d1]
            if engine == "scalar":
                nc.scalar.copy(out=dst, in_=accs[(j, d0)][:])
            else:
                nc.vector.tensor_copy(out=dst, in_=accs[(j, d0)][:])

        def store(j, c0, c1, engine=nc.sync):
            engine.dma_start(out=out[j * J_TILE : (j + 1) * J_TILE, c0:c1], in_=results[j][:, c0:c1])

        def drain(j, d0, d1, engine):
            copy_out(j, d0, d1, engine)
            store(j, d0, d1)

        zero_plane(nc.vector, 0)
        zero_plane(nc.gpsimd, 1)
        load_scales(nc.gpsimd, 1, 0, 4)
        load_lg(0, 0, 256)
        load_vs(nc.sync)
        load_lg(1, 0, 256)
        load_scales(nc.sync, 0, 0, 4)
        load_v(0, 0, 1)
        load_lg(0, 256, 384)
        load_lg(1, 256, 384)
        load_v(1, 0, 1)
        load_lg(0, 384, 512)
        load_v(0, 1, 2)
        load_v(1, 1, 2)
        load_lg(1, 384, 512)
        exponentiate(0, 0)
        exponentiate(0, 1)
        scale(0, 0)
        scale(0, 1)
        quantize(0, 0)
        quantize(0, 1)
        exponentiate(1, 0)
        scale(1, 0)
        exponentiate(1, 1)
        scale(1, 1)
        quantize(1, 0)
        quantize(1, 1)
        multiply(0, 0, 0, 256, "bank0")
        multiply(0, 0, 256, 512, "bank1")
        multiply(0, 1, 0, 512, "bank2")
        multiply(1, 0, 0, 256)
        multiply(1, 0, 256, 512)
        multiply(1, 1, 0, 512)
        exponentiate(0, 2)
        scale(0, 2)
        exponentiate(1, 2)
        scale(1, 2)
        exponentiate(0, 3)
        copy_out(0, 0, 256, "vector")
        copy_out(0, 256, 512, "scalar")
        store(0, 0, 512)
        drain(1, 0, 512, "scalar")
        quantize(0, 2)
        quantize(1, 2)
        multiply(0, 0, 512, 768, "bank3")
        multiply(0, 0, 768, 1024, "bank4")
        multiply(0, 1, 512, 1024, "bank5")
        multiply(1, 0, 512, 768)
        multiply(1, 0, 768, 1024)
        multiply(1, 1, 512, 1024)
        scale(0, 3)
        multiply(0, 2, 0, 512, "bank6")
        multiply(1, 2, 0, 512)
        multiply(0, 2, 512, 1024, "bank7")
        multiply(1, 2, 512, 1024)
        copy_out(0, 512, 768, "vector")
        quantize(0, 3)
        exponentiate(1, 3, 0, 64)
        exponentiate(1, 3, 64, 128)
        copy_out(0, 768, 1024, "scalar")
        store(0, 512, 1024)
        scale(1, 3, nc.vector, 0, 64)
        scale(1, 3, nc.vector, 64, 128)
        quantize(1, 3, 0, 64)
        quantize(1, 3, 64, 128)
        drain(1, 512, 1024, "scalar")
        drain(2, 0, 512, "scalar")
        drain(2, 512, 1024, "vector")
        multiply(0, 3, 0, 256, "bank0")
        multiply(0, 3, 256, 512, "bank1")
        multiply(0, 3, 512, 768, "bank2")
        multiply(1, 3, 0, 256)
        multiply(1, 3, 256, 512)
        multiply(0, 3, 768, 1024, "bank3")
        multiply(1, 3, 512, 768)
        multiply(1, 3, 768, 1024)
        copy_out(3, 0, 256, "vector")
        copy_out(3, 256, 512, "scalar")
        store(3, 0, 512)
        copy_out(3, 512, 768, "vector")
        copy_out(3, 768, 1024, "scalar")
        store(3, 512, 1024)
